import numpy as np, ml_dtypes
CORES = [66,74,82,90,194,202,210,218]
N = 8
import mx_ref
BF = ml_dtypes.bfloat16
def gentries(a):
    return np.ascontiguousarray(a.reshape(8, 16, -1).transpose(0, 2, 1)).reshape(8, -1)
def gtable(e):
    e = np.asarray(e); return np.ascontiguousarray(e.reshape(8, -1, 16).transpose(0, 2, 1)).reshape(128, -1).astype(np.int32)
def gcols(t, e):
    v = np.concatenate([t.reshape(8, 16, -1, 4), np.zeros((8, 16, 1, 4), BF)], axis=2)
    return np.ascontiguousarray(np.stack([v[g][:, e[g]] for g in range(8)])).reshape(128, -1)
def tile(rs):
    return np.stack(rs, axis=2).reshape(128, -1).astype(BF)
def pick(q, e):
    c = np.concatenate([q[0].reshape(128, -1, 4), np.zeros((128, 1, 4), np.uint8)], axis=1); s = np.concatenate([q[1], np.ones((16, 1), np.uint8)], axis=1)
    return (np.ascontiguousarray(c[:, e].reshape(128, -1)), np.ascontiguousarray(s[:, e]))
def join(*qs):
    return (np.concatenate([q[0] for q in qs], axis=1), np.concatenate([q[1] for q in qs], axis=1))
def put(q, e, v):
    c, s = q[0].reshape(128, -1, 4).copy(), q[1].copy(); c[:, e] = v[0].reshape(128, -1, 4); s[:, e] = v[1]
    return (c.reshape(128, -1), s)
def pk(c, s):
    return (np.ascontiguousarray(c), mx_ref.live(s))
def emit(q):
    return q[0], q[1]
def packed(v, rng):
    q = [mx_ref.quantize(np.ascontiguousarray(v[r])) for r in range(N)]
    return np.stack([a for a, b in q]), np.stack([mx_ref.plane(b, rng) for a, b in q])
def values_of_codes():
    e, c = np.zeros((128, 128, 4), np.float32), np.zeros((128, 2, 4), np.uint8)
    e[np.arange(128), np.arange(128), 0] = 1
    c[:127, :, 0] = np.arange(256).reshape(2, 128).T[:127]
    return mx_ref.matmul(mx_ref.quantize(e.reshape(128, 512).astype(BF)), (c.reshape(128, 8), np.full((16, 2), 127, np.uint8))).T.reshape(-1).astype(np.float64)
CODE_VALUE, SCALE_VALUE = values_of_codes(), 2.0 ** (np.arange(256) - 127.0)
def decode(q):
    return (CODE_VALUE[q[0]].reshape(16, 8, -1, 4) * SCALE_VALUE[q[1]][:, None, :, None] + 0.0).reshape(128, -1).astype(np.float32)
def f(rng, *shape):
    return mx_ref.flush((rng.standard_normal(shape, dtype=np.float32) * np.exp2(rng.integers(-2, 3, shape[:-1] + (1,)))).astype(BF))
def wide(rng, *shape, cols=0):
    v = rng.standard_normal(shape, dtype=np.float32) * np.exp2(rng.integers(-12, 13, shape)).astype(np.float32)
    if cols: v *= np.repeat(np.exp2(rng.integers(-cols, cols + 1, shape[:-2] + (1, shape[-1] // 4))) * (rng.random(shape[:-2] + (1, shape[-1] // 4)) > 0.0625), 4, axis=-1).astype(np.float32)
    return mx_ref.flush(v.astype(BF))
C, HALF, FAR = 352, 176, (4, 2)
def mate(r, t):
    return r ^ FAR[t]
def swap(s, t):
    lo, hi = np.arange(HALF), np.arange(HALF, C)
    return [join(pick(s[r], lo), pick(s[mate(r, t)], hi)) for r in range(N)]
def contend(e, p):
    a, b = p[:, ::2], p[:, 1::2]
    w = np.take_along_axis(e, b, axis=1) > np.take_along_axis(e, a, axis=1)
    l = np.empty_like(p)
    l[:, ::2] = np.where(w, b, a)
    l[:, 1::2] = np.where(w, a, b)
    return l
def layer(w, q):
    return [mx_ref.matmul(pick(w, np.arange(128 * b, 128 * b + 128)), q) for b in range(4)]
def clean(v):
    v = v.astype(np.float32)
    v[np.abs(v) < np.float32(2.0 ** -16)] = 0
    return v.astype(BF)
def numbers_of(rng):
    return {"x": clean(f(rng, N, 128, 4 * C)), "u": np.array(f(rng, N, 128, 512)), "v": np.array(f(rng, N, 128, 512))}
def wirings(rng):
    return {k: np.stack([gtable(np.stack([rng.permutation(C) for g in range(8)])) for r in range(N)]) for k in ("p0", "p1")}
def layers(rng, w, z):
    wc, ws = packed(np.stack([w] * N), rng)
    zc, zs = packed(np.stack([z] * N), rng)
    return {"wc": wc, "ws": ws, "zc": zc, "zs": zs}
def still(rng, k=1.0):
    w = np.zeros((128, 4, 128, 4), np.float32)
    i = np.arange(128)
    for b in range(4): w[i, b, i, b] = 32
    w = w.reshape(128, 2048)
    return layers(rng, w.astype(BF), (w * np.float32(k)).astype(BF))
def signs(rng):
    return np.stack([rng.permutation(8) % 2 * 2.0 - 1.0 for r in range(N)])
def pairs(rng, o):
    w = []
    for g in range(8):
        k = o[g].reshape(HALF, 2)[rng.permutation(HALF)]
        w.append(np.where(rng.integers(0, 2, (HALF, 1)) == 1, k[:, ::-1], k).reshape(-1))
    return np.stack(w)
def setup_inputs(rng):
    return {**numbers_of(rng), **wirings(rng), **layers(rng, np.array(f(rng, 128, 2048)), np.array(f(rng, 128, 2048)))}
def setup_inputs_ties(rng):
    d = numbers_of(rng)
    e = int(rng.integers(N))
    x = d["x"].reshape(N, 8, 16, C, 4)
    a = x[0][:, :8, :3].copy()
    a[:, :, 2] = 0
    for r in range(N):
        k = np.zeros(C, int) if r in (e, mate(e, 0)) else rng.permutation(C) % 3
        x[r][:, :8] = a[:, :, k]
    x[mate(e, 1)] = 0
    u = d["u"].reshape(N, 8, 16, 128, 4)
    for t in range(2): u[:, :, 8:, t::16] = 0
    w = np.array(f(rng, 128, 2048)).reshape(8, 16, 4, 8, 16, 4)
    w[:, 8:, :, :, :8] = 0
    return {"x": x.reshape(N, 128, 4 * C), "u": u.reshape(N, 128, 512), "v": d["v"], **wirings(rng), **layers(rng, w.reshape(128, 2048), np.array(f(rng, 128, 2048)))}
def setup_inputs_near(rng):
    d = numbers_of(rng)
    x = d["x"].astype(np.float32).reshape(N, 8, 16, C, 4)
    s = np.arange(C) // 2
    g = ((s[:, None] >> np.arange(8)) & 1) * np.exp2(np.arange(8) - 22.0)
    x[:, :, 0] = 0
    x[:, :, 0, :, 0] = 1
    x[:, :, 8] = g[:, :4]
    x[:, :, 9] = g[:, 4:]
    x[:, :, 10:] = rng.integers(4, 8, (N, 8, 6, C, 4)) * rng.choice([-1.0, 1.0], (N, 8, 6, C, 4)) * 2.0 ** -20
    one = int(rng.integers(8))
    x[:, one, 1:8] = 0
    x[:, one, 1, :, 0] = 1.75
    x[:, one, 2:4] = np.exp2(-np.arange(11.0, 19.0)).reshape(2, 1, 4)
    u = d["u"].reshape(N, 128, 128, 4)
    for t in range(2):
        u[:, :, t::16] = 0
        c = np.stack([np.exp2(-4.0 * rng.permutation(8)) for r in range(N)])
        k = (signs(rng) * c).astype(np.float32).astype(BF)
        c = c.astype(np.float32).astype(BF)
        for h in range(8):
            u[:, 16 * h, 16 * h + t, 0] = k[:, h]
            u[:, 16 * h + 8:16 * h + 10, 16 * h + t] = c[:, h][:, None, None]
    first = [pairs(rng, np.stack([np.roll(np.arange(C), -int(k)) for k in rng.permutation(8) % 2])) for r in range(N)]
    mixed = [s[contend(np.tile(s, (8, 1)), first[r])] + s for r in range(N)]
    second = []
    for r in range(N):
        k = np.concatenate([mixed[r][:, :HALF], mixed[mate(r, 1)][:, HALF:]], axis=1)
        second.append(pairs(rng, np.argsort(k, axis=1, kind="stable")))
    return {"x": x.reshape(N, 128, 4 * C).astype(BF), "u": u.reshape(N, 128, 512), "v": d["v"], "p0": np.stack([gtable(k) for k in first]), "p1": np.stack([gtable(k) for k in second]), **still(rng, 1.125)}
def setup_inputs_huge(rng):
    d = numbers_of(rng)
    x = 2.0 ** 30 * (0.6 + 0.4 * rng.random((N, 128, 4 * C)))
    u = d["u"].reshape(N, 128, 128, 4)
    for t in range(2):
        a = 2.0 ** 30 * (1 - 0.25 * rng.random((N, 128, 8, 4))) * signs(rng)[:, None, :, None]
        u[:, :, t::16] = a.astype(np.float32).astype(BF)
    return {"x": x.astype(np.float32).astype(BF), "u": u.reshape(N, 128, 512), "v": d["v"], **wirings(rng), **still(rng)}
def setup_inputs_spread(rng):
    d = setup_inputs(rng)
    d["x"] = clean(wide(rng, N, 128, 4 * C, cols=10))
    return d
def check_inputs(d):
    b = []
    for k in ("x", "u", "v"):
        a = np.abs(d[k].astype(np.float32))
        if not (np.isfinite(a).all() and ((a == 0) | (a >= 2.0 ** -30) & (a <= 2.0 ** 30)).all()): b.append("a value of " + k)
    for k in ("p0", "p1"):
        if any((np.sort(gentries(a), axis=1) != np.arange(C)).any() for a in d[k]): b.append("a group of " + k + " hasn't every number once")
    for k in ("wc", "zc"):
        if (d[k] != d[k][:1]).any(): b.append(k + " differs between ranks")
    for k in ("ws", "zs"):
        s = [mx_ref.live(p) for p in d[k]]
        if any((p != s[0]).any() for p in s): b.append(k + " differs between ranks")
    return b
def reference(x, u, v, p0, p1, wc, ws, zc, zs):
    w, z = pk(wc[0], ws[0]), pk(zc[0], zs[0])
    qu = [mx_ref.quantize(u[r]) for r in range(N)]
    now = [mx_ref.quantize(x[r]) for r in range(N)]
    kept = [[], []]
    for t in range(2):
        now = swap(now, t)
        for r in range(N):
            e = mx_ref.matmul(qu[r], now[r])[t::16] + np.float32(0.0)
            l = contend(e, gentries((p0, p1)[t][r]))
            kept[t].append(l)
            d = decode(now[r])
            p = ((gcols(d.astype(BF), l).astype(np.float32) + d) * np.float32(0.5)).astype(BF)
            now[r] = mx_ref.quantize(tile([np.maximum(a, np.float32(0.0)) * np.float32(0.03125) for a in layer(w, mx_ref.quantize(p))]))
    for t in (1, 0):
        for r in range(N):
            g = tile([a * np.float32(0.03125) for a in layer(z, now[r])])
            now[r] = mx_ref.quantize(gcols(g, np.argsort(kept[t][r], axis=1)))
        now = swap(now, t)
    y, ol = np.zeros((N, 128, C), np.float32), np.zeros((N, 8, 2 * C), np.float32)
    oc, osc = np.zeros((N, 128, 4 * C), np.uint8), np.zeros((N, 16, C), np.uint8)
    for r in range(N):
        y[r] = mx_ref.matmul(mx_ref.quantize(v[r]), now[r])
        ol[r] = np.concatenate([kept[0][r], kept[1][r]], axis=1)
        oc[r], osc[r] = emit(now[r])
    return {"y": y, "ol": ol, "oc": oc, "osc": osc}

@@ -1,0 +1,431 @@
+from concourse.mybir import dt, AluOpType, ActivationFunctionType
+
+C, HALF, FAR = 352, 176, (4, 2)
+NA = 192
+NPRE = 2
+HY = (2, 3)
+BIG = 2.0 ** 40
+F32, BF, I32, U16, Q4, U8 = "float32", "bfloat16", "int32", "uint16", "float8_e4m3fn_x4", "uint8"
+
+SCRATCH = {}
+for _n, _w in (("xt", 4 * C), ("ut", 512), ("vt", 512), ("z0", 516), ("z1", 516), ("dh0", 4 * C), ("dh1", 4 * C),
+               ("dc0", 4 * C), ("dc1", 4 * C), ("tm0", 4 * C), ("tm1", 4 * C), ("mp0", 4 * C), ("mp1", 4 * C),
+               ("mh0", 4 * C), ("mh1", 4 * C), ("mg0", 4 * C), ("mg1", 4 * C), ("mx0", 4 * C), ("mx1", 4 * C)):
+    SCRATCH[_n] = ("sbuf", [128, _w], BF)
+for _n, _w in (("xi", 64), ("xo", 80), ("iv", 132), ("pcol", 4), ("cc", 4), ("ta", 32), ("tb", 32), ("k16", 32),
+               ("kw", 2 * C), ("ki", HALF), ("wb", 2 * C), ("so", 2 * C), ("cnt", C), ("pf", 64), ("pt", 64),
+               ("pu", 64), ("pw", 64), ("df", 44), ("e0", C), ("e1", C), ("eg0", C), ("eg1", C), ("sc0", C),
+               ("sc1", C), ("r0", C), ("r1", C), ("wd", C), ("wg", C), ("sg", C), ("tg", 24), ("lf", 2 * C), ("yb", C)):
+    SCRATCH[_n] = ("sbuf", [128, _w], F32)
+SCRATCH["pi"] = ("sbuf", [128, 44], I32)
+for _n, _w in (("o16", 38), ("p16", 44), ("l0", 24), ("l0c", 22), ("l1", 22), ("n0", 24), ("n1", 24), ("q16", 22)):
+    SCRATCH[_n] = ("sbuf", [128, _w], U16)
+for _n, _w in (("u", 128), ("up", 256), ("v", 128), ("w", 512), ("z", 512), ("e", 512), ("s0", C), ("o0", HALF),
+               ("m0", C), ("o1", HALF), ("s1", C), ("m1", C), ("h1", C), ("s2", C), ("o2", HALF), ("s3", C),
+               ("o3", HALF)):
+    SCRATCH["c_" + _n] = ("sbuf", [128, _w], Q4)
+    SCRATCH["s_" + _n] = ("sbuf", [128, _w], U8)
+for _k in range(8):
+    SCRATCH["ps%d" % _k] = ("psum", [128, 512], F32)
+
+SEMAPHORES = (["kv", "ka", "kp", "kg", "go"] + ["arr%d" % k for k in range(4)] + ["left%d" % k for k in range(4)]
+              + ["d%d" % k for k in range(12)] + ["outs", "outa"])
+
+
+def _flat(x, out):
+    for d in x:
+        if isinstance(d, (list, tuple)):
+            _flat(d, out)
+        elif d is not None:
+            out.append(d)
+    return out
+
+
+def rank_program(g, core, T, topo):
+    rank = T.rank_of(core)
+    if rank is None:
+        return
+    ALU, ACT = AluOpType, ActivationFunctionType
+    queue = {"v": g.vector, "a": g.scalar, "p": g.tensor, "g": g, "s": g.sync}
+    ops = []
+
+    def op(eng, fn, *deps):
+        o = {"eng": eng, "fn": fn, "deps": _flat(deps, []), "sem": "k" + eng, "kind": "c", "used": False}
+        ops.append(o)
+        return o
+
+    dmas = [0]
+
+    def dma(eng, out, in_, *deps, sem=None):
+        if sem is None:
+            sem = "d%d" % dmas[0]
+            dmas[0] += 1
+        o = op(eng, lambda q: q.dma_start(out, in_), *deps)
+        o.update(sem=sem, kind="d", used=True)
+        return o
+
+    def event(sem, val):
+        return {"sem": sem, "val": val, "clock": {sem: val}, "kind": "e", "used": True}
+
+    def pair(name, a, b):
+        return T["c_" + name][:, a:b], T["s_" + name][:, a:b]
+
+    def quant(name, a, n, tile, *deps):
+        c, s = pair(name, a, a + n)
+        return op("v", lambda q: q.quantize_mx(c, s, tile), *deps)
+
+    free = [None] * 8
+
+    def mm(bank, lhs, rhs, n, *deps):
+        out = T["ps%d" % bank][:, 0:n]
+        return op("p", lambda q: q.matmul_mx(out, lhs[0], lhs[1], rhs[0], rhs[1], True, True), free[bank], *deps)
+
+    def evac(eng, bank, n, out, scale, relu, dep):
+        src = T["ps%d" % bank][:, 0:n]
+        if eng == "a":
+            f = ACT.Relu if relu else ACT.Copy
+            o = op("a", lambda q: q.activation(out, src, f, scale=scale), dep)
+        elif relu:
+            o = op("v", lambda q: q.tensor_scalar(out, src, 0.0, scale, ALU.max, ALU.mult), dep)
+        elif scale == 1.0:
+            o = op("v", lambda q: q.tensor_copy(out, src), dep)
+        else:
+            o = op("v", lambda q: q.tensor_scalar(out, src, scale, None, ALU.mult), dep)
+        free[bank] = o
+        return o
+
+    def copy(eng, out, in_, *deps):
+        if eng == "a":
+            return op("a", lambda q: q.activation(out, in_, ACT.Copy), *deps)
+        return op("v", lambda q: q.tensor_copy(out, in_), *deps)
+
+    def ts(out, in0, s1, s2, o0, o1, *deps):
+        if o1 is None:
+            return op("v", lambda q: q.tensor_scalar(out, in0, s1, None, o0), *deps)
+        return op("v", lambda q: q.tensor_scalar(out, in0, s1, s2, o0, o1), *deps)
+
+    def tt(out, in0, in1, o, *deps):
+        return op("v", lambda q: q.tensor_tensor(out, in0, in1, o), *deps)
+
+    def scan(out, k, x, *deps):
+        return op("v", lambda q: q.tensor_tensor_scan(out, k, x, 0.0, ALU.mult, ALU.add), *deps)
+
+    def iota(out, pattern, base, cm):
+        return op("g", lambda q: q.iota(out, pattern, base, cm, allow_small_or_imprecise_dtypes=True))
+
+    def send(k, src, dst, t, dep):
+        d = FAR[t]
+        peer = T.cores[rank + d if (rank // d) % 2 == 0 else rank - d]
+        rid, pid = topo.addr(peer, core)
+        mask = topo.mask(core, peer)
+        n = 2 * len(topo.engines(core, peer))
+        sc, ss = pair(src, 0, HALF)
+        dc, ds = pair(dst, HALF, C)
+        arr, left = T.sem["arr%d" % k], T.sem["left%d" % k]
+        a = op("g", lambda q: q.remote_dma(dc.bitcast(dt.uint8), sc.bitcast(dt.uint8), arr, left, pid, rid, mask), dep)
+        b = op("g", lambda q: q.remote_dma(ds, ss, arr, left, pid, rid, mask))
+        a["kind"] = b["kind"] = "r"
+        return event("arr%d" % k, n), event("left%d" % k, n)
+
+    W = [pair("w", 128 * b, 128 * b + 128) for b in range(4)]
+    Z = [pair("z", 128 * b, 128 * b + 128) for b in range(4)]
+    E = [pair("e", 128 * b, 128 * b + 128) for b in range(4)]
+    U = [pair("up", 128 * t, 128 * t + 128) for t in range(2)]
+
+    l_xu = dma("s", T.xt[:, 4 * HALF:4 * C], T.x[:, 4 * HALF:4 * C])
+    o = op("s", lambda q: q.sem_inc(T.sem.go, 1))
+    o["kind"] = "r"
+    l_p0 = dma("s", T.pi[:, 0:22], T.p0[:])
+    l_xl = dma("s", T.xt[:, 0:4 * HALF], T.x[:, 0:4 * HALF])
+    l_p1 = dma("a", T.pi[:, 22:44], T.p1[:], event("go", 1))
+    l_u = dma("a", T.ut[:], T.u[:])
+
+    i_a = iota(T.xi[:, 0:32], [[0, 2], [2, 8], [0, 2]], 1, 0)
+    i_b = iota(T.xi[:, 32:64], [[0, 2], [1, 16]], 0, 0)
+    i_u = iota(T.xo[:, 64:80], [[1, 2], [16, 8]], 0, 0)
+    i_v = iota(T.iv[:, 0:130], [[1, 130]], -1, 0)
+    i_p = iota(T.pcol[:, 0:1], [[0, 1]], 0, 1)
+
+    m_z0 = op("v", lambda q: q.memset(T.z0[:], 0.0))
+    m_z1 = op("v", lambda q: q.memset(T.z1[:], 0.0))
+    m_pf = op("v", lambda q: q.memset(T.pf[:, 44:64], 0.0))
+    t_x = op("v", lambda q: q.transpose(T.xo[:, 0:64], T.xi[:]), i_b)
+    m_wb = op("v", lambda q: q.memset(T.wb[:, 1:2 * C:2], 0.0))
+    s1, pm = T.xo[:, 31:32], T.xo[:, 32:33]
+    c_o = copy("v", T.o16[:], T.xo[:, 42:80], t_x, i_u)
+    ts(T.ta[:, 0:16], T.iv[:, 1:17], s1, BIG, ALU.is_equal, ALU.mult, t_x, i_v)
+    ts(T.tb[:, 0:16], T.iv[:, 2:18], s1, None, ALU.not_equal, None)
+    ts(T.ta[:, 16:32], T.iv[:, 0:16], pm, BIG, ALU.is_equal, ALU.mult)
+    k4 = ts(T.tb[:, 16:32], T.iv[:, 1:17], pm, None, ALU.not_equal, None)
+    c_c = ts(T.cc[:, 0:2], T.xo[:, 31:33], 15.0, 1.0 / BIG, ALU.is_equal, ALU.max)
+    k16 = tt(T.k16[:], T.ta[:], T.tb[:], ALU.max, k4)
+    cw, ci = T.cc[:, 0:1], T.cc[:, 1:2]
+    e1 = ts(T.z0[:, 2:514:4], T.iv[:, 1:129], T.pcol[:, 0:1], 0.5, ALU.is_equal, ALU.mult, i_p, m_z0)
+    e2 = ts(T.z1[:, 3:515:4], T.iv[:, 1:129], T.pcol[:, 0:1], 0.5, ALU.is_equal, ALU.mult, m_z1)
+    q_e = []
+    for b in range(5):
+        if b == NPRE:
+            q_xu = quant("o0", 0, HALF, T.xt[:, 4 * HALF:4 * C], l_xu)
+            arr0, left0 = send(0, "o0", "s0", 0, q_xu)
+        if b < 4:
+            a = 2 - 2 * (b // 2)
+            q_e.append(quant("e", 128 * b, 128, (T.z0, T.z1)[b % 2][:, a:a + 512], e1, e2))
+    cnt = []
+    for a, n in ((0, 128), (128, 128), (256, 96)):
+        cnt.append(op("a", lambda q, a=a, n=n: q.activation(T.cnt[:, a:a + n], T.iv[:, 1:1 + n], ACT.Identity,
+                                                           bias=float(512 + a)), i_v))
+    kw0 = copy("a", T.kw[:, 0:C], T.k16[:, 0:16].indirect(T.o16[:, 0:22]), k16, c_o)
+    ki = copy("a", T.ki[:], T.k16[:, 16:32].indirect(T.o16[:, 0:11]))
+    kw1 = copy("a", T.kw[:, C:2 * C], T.kw[:, 0:C], kw0)
+    p_f = copy("v", T.pf[:, 0:44], T.pi[:], l_p0, l_p1, m_pf)
+    p16 = copy("v", T.p16[:], T.pi[:])
+    p_t = op("v", lambda q: q.transpose(T.pt[:], T.pf[:]), p_f)
+    copy("v", T.pu[:, 0:64:2], T.pt[:, 1:64:2], p_t)
+    w_b = copy("v", T.pu[:, 1:64:2], T.pt[:, 0:64:2])
+    q_xl = quant("s0", 0, HALF, T.xt[:, 0:4 * HALF], l_xl)
+    p_w = op("v", lambda q: q.transpose(T.pw[:], T.pu[:]), w_b)
+    q_u = quant("u", 0, 128, T.ut[:], l_u)
+    p_d = tt(T.df[:], T.pw[:, 0:44], T.pf[:, 0:44], ALU.subtract, p_w)
+    uo = T.o16[:, 22:38]
+    pk_c = op("v", lambda q: q.tensor_copy(T.c_up[:].bitcast(dt.uint32), T.c_u[:].bitcast(dt.uint32).indirect(uo)),
+              q_u, c_o)
+    kslot = ts(T.kw[:, 15:2 * C:16], T.df[:], cw, None, ALU.mult, None, p_d, kw1, c_c)
+    wslot = copy("a", T.wb[:, 15:2 * C:16], T.pf[:, 0:44], p_f, m_wb)
+
+    def unpack(t, S, a, banks, dep):
+        rhs = pair(S, a, a + HALF)
+        sc = mm(banks[0], U[t], rhs, HALF, dep)
+        return sc, [mm(banks[1 + b], E[b], rhs, HALF) if a == 0 or b < HY[t]
+                    else mm(banks[1 + b], E[b], pair(S, 0, C), C) for b in range(4)]
+
+    def number(eng, name, t, a, b, banks, mms):
+        lo = a if b >= HY[t] else 0
+        o = copy(eng, T[name % t][:, C * b + a:C * b + a + HALF], T["ps%d" % banks[1 + b]][:, lo:lo + HALF], mms[b])
+        free[banks[1 + b]] = o
+        return o
+
+    def upper(plan, t, banks, mms, more=None):
+        d, c, x = [None] * 4, [None] * 4, None
+        for w in plan.split():
+            if w == "g":
+                x = more()
+            elif w[0] == "d":
+                d[int(w[1])] = number("a", "dh%d", t, HALF, int(w[1]), banks, mms)
+            elif int(w[1]) < HY[t]:
+                c[int(w[1])] = number("a", "dc%d", t, HALF, int(w[1]), banks, mms)
+        return d, c, x
+
+    def both(b):
+        return [number("a", k, 0, 0, b, bk, dm) for k in (("dh%d", "dc%d") if b < HY[0] else ("dh%d",))]
+
+    bk = [0, 1, 2, 3, 4]
+    dm = [mm(bk[1 + b], E[b], pair("s0", 0, HALF), HALF, q_xl, q_e) for b in range(4)]
+    d0l = [both(b) for b in range(2)]
+    pk_s = copy("a", T.s_up[:], T.s_u[:].indirect(uo), q_u, c_o)
+    d0l += [both(b) for b in range(2, 4)]
+    e0l = evac("a", bk[0], HALF, T.e0[:, 0:HALF], 1.0, False, mm(bk[0], U[0], pair("s0", 0, HALF), HALF, pk_c, pk_s))
+    sct1 = copy("v", T.sc1[:].indirect(T.p16[:, 22:44]), T.cnt[:], p16, cnt)
+
+    l_ws = dma("s", T.s_w[:], T.ws[:], left0)
+    l_wc = dma("s", T.c_w[:].bitcast(dt.uint8), T.wc[:])
+
+    def switch(t, eg, a, b, dep):
+        return tt(T.wb[:, C * t + a:C * t + b:2], eg[:, a + 1:b:2], eg[:, a:b:2], ALU.is_gt, dep, wslot)
+
+    def places(t, a, b, dep):
+        a, b = C * t + a, C * t + b
+        return scan(T.so[:, a:b], T.kw[:, a:b], T.wb[:, a:b], dep, kslot)
+
+    def fetch(t, off, a, n, dep, *per):
+        return [None] * HY[t] + [copy("a", T["tm%d" % t][:, C * b + a:C * b + a + n],
+                                      T["dh%d" % t][:, C * b:C * b + C].indirect(off), dep, [d[b] for d in per])
+                                 for b in range(HY[t], 4)]
+
+    def mix(t, off, a, n, b, banks, got, *deps):
+        out = T["mp%d" % t][:, 4 * a + b:4 * (a + n):4]
+        if b < HY[t]:
+            return tt(out, T["dh%d" % t][:, C * b:C * b + C].indirect(off), T["dc%d" % t][:, C * b + a:C * b + a + n],
+                      ALU.add, *deps)
+        o = tt(out, T["tm%d" % t][:, C * b + a:C * b + a + n], T["ps%d" % banks[1 + b]][:, a:a + n], ALU.add, got[b])
+        free[banks[1 + b]] = o
+        return o
+
+    bk = [5, 6, 7, 0, 1]
+    sc, dm = unpack(0, "s0", HALF, bk, arr0)
+    e0u = evac("v", bk[0], HALF, T.e0[:, HALF:C], 1.0, False, sc)
+    d0u, c0u, _ = upper("d0 c0 d1 c1 d2 d3 c2 c3", 0, bk, dm)
+    ga = copy("v", T.eg0[:, 160:C], T.e0[:].indirect(T.p16[:, 10:22]), e0u, e0l, p16)
+    wa = switch(0, T.eg0, 160, C, ga)
+    sa = places(0, 160, C, wa)
+    l0u = copy("v", T.l0[:, 12:23], T.so[:, HALF + 15:C:16], sa)
+    got = fetch(0, T.l0[:, 12:23], HALF, HALF, l0u, d0u, d0l)
+    gb = copy("a", T.eg0[:, 0:160], T.e0[:].indirect(T.p16[:, 0:10]), e0u, e0l, p16)
+    mu = [mix(0, T.l0[:, 12:23], HALF, HALF, b, bk, got, l0u, d0u[b], c0u[b], d0l[b]) for b in range(4)]
+    q_pu = quant("o1", 0, HALF, T.mp0[:, 4 * HALF:4 * C], mu)
+    arr1, left1 = send(1, "o1", "m0", 1, q_pu)
+    wl = switch(0, T.eg0, 0, 160, gb)
+    scan(T.r1[:, 0:HALF], T.ki[:], T.sc1[:, 0:HALF], sct1, ki)
+    sl = places(0, 0, 160, wl)
+    r1b = scan(T.r1[:, HALF:C], T.ki[:], T.sc1[:, HALF:C])
+    l0l = copy("v", T.l0[:, 0:11], T.so[:, 15:HALF:16], sl)
+    q16 = ts(T.q16[:], T.r1[:, 15:C:16], ci, -512.0, ALU.mult, ALU.add, r1b)
+    got = fetch(0, T.l0[:, 0:11], 0, HALF, l0l)
+    ml = [mix(0, T.l0[:, 0:11], 0, HALF, b, bk, got, l0l) for b in range(4)]
+    q_pl = quant("m0", 0, HALF, T.mp0[:, 0:4 * HALF], ml)
+
+    l_zs = dma("s", T.s_z[:], T.zs[:], left1)
+    l_zc = dma("s", T.c_z[:].bitcast(dt.uint8), T.zc[:])
+    l_v = dma("s", T.vt[:], T.v[:])
+
+    def layer(M, src, a, n, banks, *deps):
+        rhs = pair(src, a, a + n)
+        return [mm(banks[b], M[b], rhs, n, *deps) for b in range(4)]
+
+    def relu(eng, H, a, n, b, banks, mms):
+        return evac(eng, banks[b], n, H[:, 4 * a + b:4 * (a + n):4], 0.03125, True, mms[b])
+
+    def plain(eng, G, a, n, b, banks, mms):
+        return evac(eng, banks[b], n, G[:, C * b + a:C * b + a + n], 0.03125, False, mms[b])
+
+    bk = [2, 3, 4, 5]
+    mms = layer(W, "m0", 0, HALF, bk, q_pl, l_ws, l_wc)
+    l0c = copy("v", T.l0c[:], T.so[:, 15:C:16], sl)
+    hs = [relu("av"[b % 2], T.mh0, 0, HALF, b, bk, mms) for b in range(4)]
+    q_hl = quant("s1", 0, HALF, T.mh0[:, 0:4 * HALF], hs)
+    bk = [6, 7, 0, 1, 2]
+    sc, dm = unpack(1, "s1", 0, bk, q_hl)
+    e1l = evac("a", bk[0], HALF, T.e1[:, 0:HALF], 1.0, False, sc)
+    bu = [3, 4, 5, 6]
+    mms = layer(W, "m0", HALF, HALF, bu, arr1)
+    d1l = [number("av"[b % 2], "dh%d", 1, 0, b, bk, dm) for b in range(4)]
+    hs = [relu("va"[b % 2], T.mh0, HALF, HALF, b, bu, mms) for b in range(4)]
+    q_hu = quant("s1", HALF, HALF, T.mh0[:, 4 * HALF:4 * C], hs)
+
+    NB, KA = C - NA, NA // 16
+    bk = [7, 0, 1, 2, 3]
+    sc, dm = unpack(1, "s1", HALF, bk, q_hu)
+    c1l = [copy("v", T.dc1[:, C * b:C * b + HALF], T.dh1[:, C * b:C * b + HALF], d1l[b]) for b in range(HY[1])]
+    c1l += [None] * 4
+    e1u = evac("v", bk[0], HALF, T.e1[:, HALF:C], 1.0, False, sc)
+    d1u, c1u, gb = upper("d0 g c0 d1 c1 d2 d3 c2 c3", 1, bk, dm, lambda: copy(
+        "a", T.eg1[:, NA:C], T.e1[:].indirect(T.p16[:, 22 + KA:44]), e1u, e1l))
+    ga = copy("v", T.eg1[:, 0:NA], T.e1[:].indirect(T.p16[:, 22:22 + KA]), e1u, e1l)
+    wa = switch(1, T.eg1, 0, NA, ga)
+    wb = switch(1, T.eg1, NA, C, gb)
+    sa = places(1, 0, NA, wa)
+    sb = places(1, NA, C, wb)
+    l1a = copy("v", T.l1[:, 0:KA], T.so[:, C + 15:C + NA:16], sa)
+    l1b = copy("v", T.l1[:, KA:22], T.so[:, C + NA + 15:2 * C:16], sb)
+    gta = fetch(1, T.l1[:, 0:KA], 0, NA, l1a, d1u, d1l)
+    gtb = fetch(1, T.l1[:, KA:22], NA, NB, l1b)
+    ma = [mix(1, T.l1[:, 0:KA], 0, NA, b, bk, gta, l1a, d1u[b], c1l[b], c1u[b]) for b in range(4)]
+    mb = [mix(1, T.l1[:, KA:22], NA, NB, 0, bk, gtb, l1b)]
+    q_pa = quant("m1", 0, NA, T.mp1[:, 0:4 * NA], ma)
+    copy("a", T.wd[:, 0:C:2], T.wb[:, C:2 * C:2], wa, wb)
+    wd1 = op("a", lambda q: q.activation(T.wd[:, 1:C:2], T.wb[:, C:2 * C:2], ACT.Copy, scale=-1.0))
+    wgu = copy("a", T.wg[:, 160:C], T.wd[:].indirect(T.q16[:, 10:22]), wd1, q16)
+    ba, bz = [4, 5, 6, 7], [0, 1, 2, 3]
+    mms = layer(W, "m1", 0, NA, ba, q_pa)
+    ha = [relu("a", T.mh1, 0, NA, b, ba, mms) for b in range(3)]
+    mb += [mix(1, T.l1[:, KA:22], NA, NB, b, bk, gtb, l1b) for b in range(1, 4)]
+    ha.append(relu("v", T.mh1, 0, NA, 3, ba, mms))
+    q_pb = quant("m1", NA, NB, T.mp1[:, 4 * NA:4 * C], mb)
+    q_ha = quant("h1", 0, NA, T.mh1[:, 0:4 * NA], ha)
+    su = scan(T.sg[:, HALF:C], T.ki[:], T.wg[:, HALF:C], wgu)
+    mwb = layer(W, "m1", NA, NB, ba, q_pb)
+    mza = layer(Z, "h1", 0, NA, bz, q_ha, l_zs, l_zc)
+    hb = [relu("av"[b % 2], T.mh1, NA, NB, b, ba, mwb) for b in range(4)]
+    q_hb = quant("h1", NA, NB, T.mh1[:, 4 * NA:4 * C], hb)
+    tu = tt(T.tg[:, 12:23], T.sg[:, HALF + 15:C:16], T.r1[:, HALF + 15:C:16], ALU.add, su)
+    g1a = [plain("av"[b % 2], T.mg1, 0, NA, b, bz, mza) for b in range(4)]
+    n1u = ts(T.n1[:, 12:23], T.tg[:, 12:23], ci, -512.0, ALU.mult, ALU.add, tu)
+    mzb = layer(Z, "h1", NA, NB, ba, q_hb)
+    g1b = [plain("av"[b % 2], T.mg1, NA, NB, b, ba, mzb) for b in range(4)]
+
+    def undo(X, G, off, a, ga, gb, dep):
+        return [copy("av"[b % 2], X[:, 4 * a + b:4 * (a + HALF):4], G[:, C * b:C * b + C].indirect(off),
+                     ga[b], gb[b], dep) for b in range(4)]
+
+    xu = undo(T.mx1, T.mg1, T.n1[:, 12:23], HALF, g1a, g1b, n1u)
+    q_x = quant("o2", 0, HALF, T.mx1[:, 4 * HALF:4 * C], xu)
+    arr2, left2 = send(2, "o2", "s2", 1, q_x)
+
+    wgl = copy("a", T.wg[:, 0:160], T.wd[:].indirect(T.q16[:, 0:10]))
+    sl = scan(T.sg[:, 0:HALF], T.ki[:], T.wg[:, 0:HALF], wgl)
+    sct0 = copy("v", T.sc0[:].indirect(T.l0[:, 0:11]), T.cnt[:, 0:HALF])
+    tl = tt(T.tg[:, 0:11], T.sg[:, 15:HALF:16], T.r1[:, 15:HALF:16], ALU.add, sl)
+    n1l = ts(T.n1[:, 0:11], T.tg[:, 0:11], ci, -512.0, ALU.mult, ALU.add, tl)
+    xl = undo(T.mx1, T.mg1, T.n1[:, 0:11], 0, g1a, g1b, n1l)
+    q_x = quant("s2", 0, HALF, T.mx1[:, 0:4 * HALF], xl)
+    bk = [0, 1, 2, 3]
+    mms = layer(Z, "s2", 0, HALF, bk, q_x)
+    sct0 = copy("v", T.sc0[:].indirect(T.l0[:, 12:23]), T.cnt[:, HALF:C], sct0)
+    r0u = scan(T.r0[:, HALF:C], T.ki[:], T.sc0[:, HALF:C], sct0)
+    n0u = ts(T.n0[:, 12:23], T.r0[:, HALF + 15:C:16], ci, -512.0, ALU.mult, ALU.add, r0u)
+    g0l = [plain("aaav"[b], T.mg0, 0, HALF, b, bk, mms) for b in range(4)]
+    bk = [4, 5, 6, 7]
+    mms = layer(Z, "s2", HALF, HALF, bk, arr2)
+    g0u = [plain("av"[b % 2], T.mg0, HALF, HALF, b, bk, mms) for b in range(4)]
+    xu = undo(T.mx0, T.mg0, T.n0[:, 12:23], HALF, g0l, g0u, n0u)
+    q_x = quant("o3", 0, HALF, T.mx0[:, 4 * HALF:4 * C], xu)
+    arr3, left3 = send(3, "o3", "s3", 0, q_x)
+
+    r0l = scan(T.r0[:, 0:HALF], T.ki[:], T.sc0[:, 0:HALF], sct0)
+    q_v = quant("v", 0, 128, T.vt[:], l_v)
+    n0l = ts(T.n0[:, 0:11], T.r0[:, 15:HALF:16], ci, -512.0, ALU.mult, ALU.add, r0l)
+    f0 = op("a", lambda q: q.activation(T.lf[:, 0:C], T.cnt[:].indirect(T.l0c[:]), ACT.Identity, bias=-512.0), l0c)
+    xl = undo(T.mx0, T.mg0, T.n0[:, 0:11], 0, g0l, g0u, n0l)
+    q_x = quant("s3", 0, HALF, T.mx0[:, 0:4 * HALF], xl)
+    f1 = op("a", lambda q: q.activation(T.lf[:, C:2 * C], T.cnt[:].indirect(T.l1[:]), ACT.Identity, bias=-512.0),
+            l1a, l1b)
+
+    V = pair("v", 0, 128)
+    yl = evac("v", 0, HALF, T.yb[:, 0:HALF], 1.0, False, mm(0, V, pair("s3", 0, HALF), HALF, q_x, q_v))
+    dma("s", T.oc[:, 0:4 * HALF], T.c_s3[:, 0:HALF].bitcast(dt.uint8), q_x, sem="outs")
+    dma("s", T.y[:, 0:HALF], T.yb[:, 0:HALF], yl, sem="outs")
+    dma("a", T.ol[:], T.lf[0:128:16, :], f0, f1, sem="outa")
+    yu = evac("v", 1, HALF, T.yb[:, HALF:C], 1.0, False, mm(1, V, pair("s3", HALF, C), HALF, arr3))
+    dma("a", T.oc[:, 4 * HALF:4 * C], T.c_s3[:, HALF:C].bitcast(dt.uint8), arr3, sem="outa")
+    for k in range(4):
+        dma("as"[k // 2], T.osc[4 * k:4 * k + 4, :], T.s_s3[32 * k:32 * k + 4, :], arr3, q_x, sem="out" + "as"[k // 2])
+    dma("s", T.y[:, HALF:C], T.yb[:, HALF:C], yu, sem="outs")
+
+    for o in ops:
+        for d in o["deps"]:
+            d["used"] = True
+    total = {}
+    for o in ops:
+        if o["kind"] == "d":
+            total[o["sem"]] = total.get(o["sem"], 0) + 16
+            o["val"] = total[o["sem"]]
+        elif o["kind"] == "c" and o["used"]:
+            total[o["sem"]] = total.get(o["sem"], 0) + 1
+            o["val"] = total[o["sem"]]
+    clock = {k: {} for k in queue}
+
+    def wait(eng, deps):
+        need = {}
+        for d in deps:
+            if d["sem"] not in need or need[d["sem"]]["val"] < d["val"]:
+                need[d["sem"]] = d
+        need = list(need.values())
+        for d in need:
+            if clock[eng].get(d["sem"], 0) >= d["val"]:
+                continue
+            if any(x is not d and x["clock"].get(d["sem"], 0) >= d["val"] for x in need):
+                continue
+            queue[eng].wait_ge(T.sem[d["sem"]], d["val"])
+        for d in need:
+            for s, v in d["clock"].items():
+                clock[eng][s] = max(clock[eng].get(s, 0), v)
+
+    for o in ops:
+        wait(o["eng"], o["deps"])
+        ins = o["fn"](queue[o["eng"]])
+        if o["kind"] != "r" and o["used"]:
+            ins.then_inc(T.sem[o["sem"]], 16 if o["kind"] == "d" else 1)
+            o["clock"] = dict(clock[o["eng"]])
+            o["clock"][o["sem"]] = o["val"]
+    wait("g", [left2, left3])
+    wait("s", [event("outs", total["outs"])])
+    wait("a", [event("outa", total["outa"])])

@@ -2,7 +2,7 @@ from concourse.mybir import dt, AluOpType, ActivationFunctionType
 
 C, HALF, FAR = 352, 176, (4, 2)
 NA = 192
-NPRE = 2
+NPRE = 1
 HY = (2, 3)
 BIG = 2.0 ** 40
 F32, BF, I32, U16, Q4, U8 = "float32", "bfloat16", "int32", "uint16", "float8_e4m3fn_x4", "uint8"
@@ -192,37 +192,37 @@ def rank_program(g, core, T, topo):
     kslot = ts(T.kw[:, 15:2 * C:16], T.df[:], cw, None, ALU.mult, None, p_d, kw1, c_c)
     wslot = copy("a", T.wb[:, 15:2 * C:16], T.pf[:, 0:44], p_f, m_wb)
 
-    def unpack(t, S, a, banks, dep):
-        rhs = pair(S, a, a + HALF)
+    def whole(t, b):
+        return t == 0 or b >= HY[t]
+
+    def unpack(t, S, banks, dep):
+        rhs = pair(S, HALF, C)
         sc = mm(banks[0], U[t], rhs, HALF, dep)
-        return sc, [mm(banks[1 + b], E[b], rhs, HALF) if a == 0 or b < HY[t]
-                    else mm(banks[1 + b], E[b], pair(S, 0, C), C) for b in range(4)]
+        return sc, [mm(banks[1 + b], E[b], pair(S, 0, C), C) if whole(t, b) else mm(banks[1 + b], E[b], rhs, HALF)
+                    for b in range(4)]
 
     def number(eng, name, t, a, b, banks, mms):
-        lo = a if b >= HY[t] else 0
+        lo = a if whole(t, b) else 0
         o = copy(eng, T[name % t][:, C * b + a:C * b + a + HALF], T["ps%d" % banks[1 + b]][:, lo:lo + HALF], mms[b])
         free[banks[1 + b]] = o
         return o
 
-    def upper(plan, t, banks, mms, more=None):
+    def upper(plan, t, banks, mms, more):
         d, c, x = [None] * 4, [None] * 4, None
         for w in plan.split():
             if w == "g":
                 x = more()
             elif w[0] == "d":
                 d[int(w[1])] = number("a", "dh%d", t, HALF, int(w[1]), banks, mms)
-            elif int(w[1]) < HY[t]:
+            else:
                 c[int(w[1])] = number("a", "dc%d", t, HALF, int(w[1]), banks, mms)
         return d, c, x
 
-    def both(b):
-        return [number("a", k, 0, 0, b, bk, dm) for k in (("dh%d", "dc%d") if b < HY[0] else ("dh%d",))]
-
     bk = [0, 1, 2, 3, 4]
     dm = [mm(bk[1 + b], E[b], pair("s0", 0, HALF), HALF, q_xl, q_e) for b in range(4)]
-    d0l = [both(b) for b in range(2)]
+    d0l = [number("a", "dh%d", 0, 0, b, bk, dm) for b in range(2)]
     pk_s = copy("a", T.s_up[:], T.s_u[:].indirect(uo), q_u, c_o)
-    d0l += [both(b) for b in range(2, 4)]
+    d0l += [number("a", "dh%d", 0, 0, b, bk, dm) for b in range(2, 4)]
     e0l = evac("a", bk[0], HALF, T.e0[:, 0:HALF], 1.0, False, mm(bk[0], U[0], pair("s0", 0, HALF), HALF, pk_c, pk_s))
     sct1 = copy("v", T.sc1[:].indirect(T.p16[:, 22:44]), T.cnt[:], p16, cnt)
 
@@ -236,14 +236,14 @@ def rank_program(g, core, T, topo):
         a, b = C * t + a, C * t + b
         return scan(T.so[:, a:b], T.kw[:, a:b], T.wb[:, a:b], dep, kslot)
 
-    def fetch(t, off, a, n, dep, *per):
-        return [None] * HY[t] + [copy("a", T["tm%d" % t][:, C * b + a:C * b + a + n],
-                                      T["dh%d" % t][:, C * b:C * b + C].indirect(off), dep, [d[b] for d in per])
-                                 for b in range(HY[t], 4)]
+    def fetch(t, h, off, a, n, dep, *per):
+        return [None] * h + [copy("a", T["tm%d" % t][:, C * b + a:C * b + a + n],
+                                  T["dh%d" % t][:, C * b:C * b + C].indirect(off), dep, [d[b] for d in per])
+                             for b in range(h, 4)]
 
     def mix(t, off, a, n, b, banks, got, *deps):
         out = T["mp%d" % t][:, 4 * a + b:4 * (a + n):4]
-        if b < HY[t]:
+        if got[b] is None:
             return tt(out, T["dh%d" % t][:, C * b:C * b + C].indirect(off), T["dc%d" % t][:, C * b + a:C * b + a + n],
                       ALU.add, *deps)
         o = tt(out, T["tm%d" % t][:, C * b + a:C * b + a + n], T["ps%d" % banks[1 + b]][:, a:a + n], ALU.add, got[b])
@@ -251,25 +251,25 @@ def rank_program(g, core, T, topo):
         return o
 
     bk = [5, 6, 7, 0, 1]
-    sc, dm = unpack(0, "s0", HALF, bk, arr0)
+    sc, dm = unpack(0, "s0", bk, arr0)
     e0u = evac("v", bk[0], HALF, T.e0[:, HALF:C], 1.0, False, sc)
-    d0u, c0u, _ = upper("d0 c0 d1 c1 d2 d3 c2 c3", 0, bk, dm)
+    d0u, c0u, gb = upper("d0 g d1 d2 d3", 0, bk, dm, lambda: copy(
+        "a", T.eg0[:, 0:160], T.e0[:].indirect(T.p16[:, 0:10]), e0u, e0l, p16))
     ga = copy("v", T.eg0[:, 160:C], T.e0[:].indirect(T.p16[:, 10:22]), e0u, e0l, p16)
+    c0u[0] = copy("v", T.dc0[:, HALF:C], T.dh0[:, HALF:C], d0u[0])
     wa = switch(0, T.eg0, 160, C, ga)
+    wl = switch(0, T.eg0, 0, 160, gb)
     sa = places(0, 160, C, wa)
+    c0u[1] = copy("v", T.dc0[:, C + HALF:2 * C], T.dh0[:, C + HALF:2 * C], d0u[1])
     l0u = copy("v", T.l0[:, 12:23], T.so[:, HALF + 15:C:16], sa)
-    got = fetch(0, T.l0[:, 12:23], HALF, HALF, l0u, d0u, d0l)
-    gb = copy("a", T.eg0[:, 0:160], T.e0[:].indirect(T.p16[:, 0:10]), e0u, e0l, p16)
-    mu = [mix(0, T.l0[:, 12:23], HALF, HALF, b, bk, got, l0u, d0u[b], c0u[b], d0l[b]) for b in range(4)]
+    sl = places(0, 0, 160, wl)
+    got = fetch(0, HY[0], T.l0[:, 12:23], HALF, HALF, l0u, d0u, d0l)
+    mu = [mix(0, T.l0[:, 12:23], HALF, HALF, 0, bk, got, l0u, d0u[0], c0u[0], d0l[0])]
+    l0l = copy("v", T.l0[:, 0:11], T.so[:, 15:HALF:16], sl)
+    mu += [mix(0, T.l0[:, 12:23], HALF, HALF, b, bk, got, l0u, d0u[b], c0u[b], d0l[b]) for b in range(1, 4)]
     q_pu = quant("o1", 0, HALF, T.mp0[:, 4 * HALF:4 * C], mu)
     arr1, left1 = send(1, "o1", "m0", 1, q_pu)
-    wl = switch(0, T.eg0, 0, 160, gb)
-    scan(T.r1[:, 0:HALF], T.ki[:], T.sc1[:, 0:HALF], sct1, ki)
-    sl = places(0, 0, 160, wl)
-    r1b = scan(T.r1[:, HALF:C], T.ki[:], T.sc1[:, HALF:C])
-    l0l = copy("v", T.l0[:, 0:11], T.so[:, 15:HALF:16], sl)
-    q16 = ts(T.q16[:], T.r1[:, 15:C:16], ci, -512.0, ALU.mult, ALU.add, r1b)
-    got = fetch(0, T.l0[:, 0:11], 0, HALF, l0l)
+    got = fetch(0, 0, T.l0[:, 0:11], 0, HALF, l0l)
     ml = [mix(0, T.l0[:, 0:11], 0, HALF, b, bk, got, l0l) for b in range(4)]
     q_pl = quant("m0", 0, HALF, T.mp0[:, 0:4 * HALF], ml)
 
@@ -289,25 +289,30 @@ def rank_program(g, core, T, topo):
 
     bk = [2, 3, 4, 5]
     mms = layer(W, "m0", 0, HALF, bk, q_pl, l_ws, l_wc)
-    l0c = copy("v", T.l0c[:], T.so[:, 15:C:16], sl)
+    scan(T.r1[:, 0:HALF], T.ki[:], T.sc1[:, 0:HALF], sct1, ki)
+    r1b = scan(T.r1[:, HALF:C], T.ki[:], T.sc1[:, HALF:C])
     hs = [relu("av"[b % 2], T.mh0, 0, HALF, b, bk, mms) for b in range(4)]
     q_hl = quant("s1", 0, HALF, T.mh0[:, 0:4 * HALF], hs)
-    bk = [6, 7, 0, 1, 2]
-    sc, dm = unpack(1, "s1", 0, bk, q_hl)
-    e1l = evac("a", bk[0], HALF, T.e1[:, 0:HALF], 1.0, False, sc)
-    bu = [3, 4, 5, 6]
+    bk, bu = [6, 7, 0, 1, 2], [3, 4, 5, 6]
+    rhs = pair("s1", 0, HALF)
+    l0c = copy("v", T.l0c[:], T.so[:, 15:C:16], sl)
+    q16 = ts(T.q16[:], T.r1[:, 15:C:16], ci, -512.0, ALU.mult, ALU.add, r1b)
+    dm = [mm(bk[1 + b], E[b], rhs, HALF, q_hl) for b in range(3)]
+    d1l = [number("ava"[b], "dh%d", 1, 0, b, bk, dm) for b in range(3)]
     mms = layer(W, "m0", HALF, HALF, bu, arr1)
-    d1l = [number("av"[b % 2], "dh%d", 1, 0, b, bk, dm) for b in range(4)]
-    hs = [relu("va"[b % 2], T.mh0, HALF, HALF, b, bu, mms) for b in range(4)]
+    hs = [relu("av"[b % 2], T.mh0, HALF, HALF, b, bu, mms) for b in range(4)]
+    dm.append(mm(bk[4], E[3], rhs, HALF))
+    e1l = evac("a", 3, HALF, T.e1[:, 0:HALF], 1.0, False, mm(3, U[1], rhs, HALF))
+    d1l.append(number("a", "dh%d", 1, 0, 3, bk, dm))
     q_hu = quant("s1", HALF, HALF, T.mh0[:, 4 * HALF:4 * C], hs)
 
     NB, KA = C - NA, NA // 16
     bk = [7, 0, 1, 2, 3]
-    sc, dm = unpack(1, "s1", HALF, bk, q_hu)
+    sc, dm = unpack(1, "s1", bk, q_hu)
     c1l = [copy("v", T.dc1[:, C * b:C * b + HALF], T.dh1[:, C * b:C * b + HALF], d1l[b]) for b in range(HY[1])]
     c1l += [None] * 4
     e1u = evac("v", bk[0], HALF, T.e1[:, HALF:C], 1.0, False, sc)
-    d1u, c1u, gb = upper("d0 g c0 d1 c1 d2 d3 c2 c3", 1, bk, dm, lambda: copy(
+    d1u, c1u, gb = upper("d0 g c0 d1 c1 d2 d3 c2", 1, bk, dm, lambda: copy(
         "a", T.eg1[:, NA:C], T.e1[:].indirect(T.p16[:, 22 + KA:44]), e1u, e1l))
     ga = copy("v", T.eg1[:, 0:NA], T.e1[:].indirect(T.p16[:, 22:22 + KA]), e1u, e1l)
     wa = switch(1, T.eg1, 0, NA, ga)
@@ -316,8 +321,8 @@ def rank_program(g, core, T, topo):
     sb = places(1, NA, C, wb)
     l1a = copy("v", T.l1[:, 0:KA], T.so[:, C + 15:C + NA:16], sa)
     l1b = copy("v", T.l1[:, KA:22], T.so[:, C + NA + 15:2 * C:16], sb)
-    gta = fetch(1, T.l1[:, 0:KA], 0, NA, l1a, d1u, d1l)
-    gtb = fetch(1, T.l1[:, KA:22], NA, NB, l1b)
+    gta = fetch(1, HY[1], T.l1[:, 0:KA], 0, NA, l1a, d1u, d1l)
+    gtb = fetch(1, HY[1], T.l1[:, KA:22], NA, NB, l1b)
     ma = [mix(1, T.l1[:, 0:KA], 0, NA, b, bk, gta, l1a, d1u[b], c1l[b], c1u[b]) for b in range(4)]
     mb = [mix(1, T.l1[:, KA:22], NA, NB, 0, bk, gtb, l1b)]
     q_pa = quant("m1", 0, NA, T.mp1[:, 0:4 * NA], ma)
@@ -334,6 +339,7 @@ def rank_program(g, core, T, topo):
     su = scan(T.sg[:, HALF:C], T.ki[:], T.wg[:, HALF:C], wgu)
     mwb = layer(W, "m1", NA, NB, ba, q_pb)
     mza = layer(Z, "h1", 0, NA, bz, q_ha, l_zs, l_zc)
+    wgl = copy("a", T.wg[:, 0:160], T.wd[:].indirect(T.q16[:, 0:10]))
     hb = [relu("av"[b % 2], T.mh1, NA, NB, b, ba, mwb) for b in range(4)]
     q_hb = quant("h1", NA, NB, T.mh1[:, 4 * NA:4 * C], hb)
     tu = tt(T.tg[:, 12:23], T.sg[:, HALF + 15:C:16], T.r1[:, HALF + 15:C:16], ALU.add, su)
@@ -342,31 +348,30 @@ def rank_program(g, core, T, topo):
     mzb = layer(Z, "h1", NA, NB, ba, q_hb)
     g1b = [plain("av"[b % 2], T.mg1, NA, NB, b, ba, mzb) for b in range(4)]
 
-    def undo(X, G, off, a, ga, gb, dep):
-        return [copy("av"[b % 2], X[:, 4 * a + b:4 * (a + HALF):4], G[:, C * b:C * b + C].indirect(off),
+    def undo(engs, X, G, off, a, ga, gb, dep):
+        return [copy(engs[b], X[:, 4 * a + b:4 * (a + HALF):4], G[:, C * b:C * b + C].indirect(off),
                      ga[b], gb[b], dep) for b in range(4)]
 
-    xu = undo(T.mx1, T.mg1, T.n1[:, 12:23], HALF, g1a, g1b, n1u)
+    xu = undo("avav", T.mx1, T.mg1, T.n1[:, 12:23], HALF, g1a, g1b, n1u)
     q_x = quant("o2", 0, HALF, T.mx1[:, 4 * HALF:4 * C], xu)
     arr2, left2 = send(2, "o2", "s2", 1, q_x)
 
-    wgl = copy("a", T.wg[:, 0:160], T.wd[:].indirect(T.q16[:, 0:10]))
     sl = scan(T.sg[:, 0:HALF], T.ki[:], T.wg[:, 0:HALF], wgl)
-    sct0 = copy("v", T.sc0[:].indirect(T.l0[:, 0:11]), T.cnt[:, 0:HALF])
     tl = tt(T.tg[:, 0:11], T.sg[:, 15:HALF:16], T.r1[:, 15:HALF:16], ALU.add, sl)
     n1l = ts(T.n1[:, 0:11], T.tg[:, 0:11], ci, -512.0, ALU.mult, ALU.add, tl)
-    xl = undo(T.mx1, T.mg1, T.n1[:, 0:11], 0, g1a, g1b, n1l)
+    sct0 = copy("v", T.sc0[:].indirect(T.l0[:, 0:11]), T.cnt[:, 0:HALF])
+    xl = undo("aaav", T.mx1, T.mg1, T.n1[:, 0:11], 0, g1a, g1b, n1l)
     q_x = quant("s2", 0, HALF, T.mx1[:, 0:4 * HALF], xl)
     bk = [0, 1, 2, 3]
     mms = layer(Z, "s2", 0, HALF, bk, q_x)
     sct0 = copy("v", T.sc0[:].indirect(T.l0[:, 12:23]), T.cnt[:, HALF:C], sct0)
     r0u = scan(T.r0[:, HALF:C], T.ki[:], T.sc0[:, HALF:C], sct0)
     n0u = ts(T.n0[:, 12:23], T.r0[:, HALF + 15:C:16], ci, -512.0, ALU.mult, ALU.add, r0u)
-    g0l = [plain("aaav"[b], T.mg0, 0, HALF, b, bk, mms) for b in range(4)]
+    g0l = [plain("a", T.mg0, 0, HALF, b, bk, mms) for b in range(4)]
     bk = [4, 5, 6, 7]
     mms = layer(Z, "s2", HALF, HALF, bk, arr2)
     g0u = [plain("av"[b % 2], T.mg0, HALF, HALF, b, bk, mms) for b in range(4)]
-    xu = undo(T.mx0, T.mg0, T.n0[:, 12:23], HALF, g0l, g0u, n0u)
+    xu = undo("avav", T.mx0, T.mg0, T.n0[:, 12:23], HALF, g0l, g0u, n0u)
     q_x = quant("o3", 0, HALF, T.mx0[:, 4 * HALF:4 * C], xu)
     arr3, left3 = send(3, "o3", "s3", 0, q_x)
 
@@ -374,7 +379,7 @@ def rank_program(g, core, T, topo):
     q_v = quant("v", 0, 128, T.vt[:], l_v)
     n0l = ts(T.n0[:, 0:11], T.r0[:, 15:HALF:16], ci, -512.0, ALU.mult, ALU.add, r0l)
     f0 = op("a", lambda q: q.activation(T.lf[:, 0:C], T.cnt[:].indirect(T.l0c[:]), ACT.Identity, bias=-512.0), l0c)
-    xl = undo(T.mx0, T.mg0, T.n0[:, 0:11], 0, g0l, g0u, n0l)
+    xl = undo("avav", T.mx0, T.mg0, T.n0[:, 0:11], 0, g0l, g0u, n0l)
     q_x = quant("s3", 0, HALF, T.mx0[:, 0:4 * HALF], xl)
     f1 = op("a", lambda q: q.activation(T.lf[:, C:2 * C], T.cnt[:].indirect(T.l1[:]), ACT.Identity, bias=-512.0),
             l1a, l1b)
@@ -387,7 +392,7 @@ def rank_program(g, core, T, topo):
     yu = evac("v", 1, HALF, T.yb[:, HALF:C], 1.0, False, mm(1, V, pair("s3", HALF, C), HALF, arr3))
     dma("a", T.oc[:, 4 * HALF:4 * C], T.c_s3[:, HALF:C].bitcast(dt.uint8), arr3, sem="outa")
     for k in range(4):
-        dma("as"[k // 2], T.osc[4 * k:4 * k + 4, :], T.s_s3[32 * k:32 * k + 4, :], arr3, q_x, sem="out" + "as"[k // 2])
+        dma("aaas"[k], T.osc[4 * k:4 * k + 4, :], T.s_s3[32 * k:32 * k + 4, :], arr3, q_x, sem="out" + "aaas"[k])
     dma("s", T.y[:, HALF:C], T.yb[:, HALF:C], yu, sem="outs")
 
     for o in ops:

@@ -1,24 +1,41 @@
 from concourse.mybir import dt, AluOpType, ActivationFunctionType
 
 C, HALF, FAR = 352, 176, (4, 2)
-NA = 192
-NPRE = 1
-HY = (2, 3)
 BIG = 2.0 ** 40
 F32, BF, I32, U16, Q4, U8 = "float32", "bfloat16", "int32", "uint16", "float8_e4m3fn_x4", "uint8"
 
+PLAN = dict(d00="aaaa", d01="vaaa", d10="aavv", d11="aaaa", e="aavv", ga="avaava", m00="faaa", m01="ffaa", m10="ffaa",
+            m11="ffaa", h00="vvaa", h01="aavv", h10="aava", h11="avva", g10="vaaa", g11="vaav", g00="aaaa",
+            g01="avav", x10="vaaa", x11="vaav", x00="vvaa", x01="vava", wg="aa", y="vv", c00="gggg", c01="gggg",
+            c10="gggg", c11="gggg", first=0, wd="g")
+ORDER = """
+lxu mz1 ia go lxl lp0 lj00 lj01 lp1 lu ib mz0 iv tx iu k2 cnt0 ip k3 cnt256 k1 cnt128 k4 co k16 e2 kw0 qxu sc0 qe1 ss0
+e1 ki qe3 qxl kw1 sd001 d001 p16 mwb qe0 sct1 sd000 sd003 d000 lj10 lj11 c000 qu lws lwc cc qe2 pks pkc sd002 d002 sct2
+se00 e00 d003 wslot r1 se01 sd011 sd010 e01 sd012 sd013 pd ga00 ga01 ga02 d010 w01 kslot c010 d011 w00 d012 sn01 d013
+sn00 c011 l01 l00 m010 t013 m011 t012 m013 t002 m012 qp01 t001 sc1 m002 ss1 t003 m000 m001 m003 qp00 sw003 sw001 lzc
+lzs lv sw002 h003 sw000 h001 h002 h000 qh00 se10 sw011 sw012 e10 sw010 h011 q16 h010 h012 sw013 sd100 h013 sd101 sd102
+d100 sd103 qh01 d101 d102 c100 se11 sd111 sd110 e11 sd112 d111 sd113 ga11 c101 ga10 d103 ga12 w10 c111 d113 w11 d110
+sn10 d112 sn11 wd0 wd1 l10 l11 t103 m101 c110 t102 m100 m103 t112 m102 wg1 m111 qp10 t113 m110 sw102 wg0 sw100 sw103
+m112 sw101 h103 m113 h101 h102 h100 qp11 sg1 sw110 qh10 sw112 sw113 h110 sw111 h112 sz101 sz102 h113 sz100 h111 sz103
+g101 tg1 qh11 g102 g100 g103 sz111 sg0 sz113 g111 sz112 sz110 n11 g112 tg0 g113 x111 g110 x113 x112 x110 n10 qx11 x101
+x100 sc2 ss2 x102 qv sct00 x103 qx10 sct01 sz001 sz000 sz002 g001 sz003 g000 r0 g003 sz010 sz011 g002 sz012 n01 sz013
+n00 g010 g011 g012 g013 x011 x010 x013 x012 x002 qx01 x001 sc3 ss3 x003 x000 f11 qx00 f00 oc0 sy0 f01 y0 oy0 f10 oc1
+os2 os0 os3 os1 ol sy1 y1 oy1
+"""
+
 SCRATCH = {}
 for _n, _w in (("xt", 4 * C), ("ut", 512), ("vt", 512), ("z0", 516), ("z1", 516), ("dh0", 4 * C), ("dh1", 4 * C),
-               ("dc0", 4 * C), ("dc1", 4 * C), ("tm0", 4 * C), ("tm1", 4 * C), ("mp0", 4 * C), ("mp1", 4 * C),
+               ("tm0", 4 * C), ("tm1", 4 * C), ("dc0", 4 * C), ("dc1", 4 * C), ("mp0", 4 * C), ("mp1", 4 * C),
                ("mh0", 4 * C), ("mh1", 4 * C), ("mg0", 4 * C), ("mg1", 4 * C), ("mx0", 4 * C), ("mx1", 4 * C)):
     SCRATCH[_n] = ("sbuf", [128, _w], BF)
 for _n, _w in (("xi", 64), ("xo", 80), ("iv", 132), ("pcol", 4), ("cc", 4), ("ta", 32), ("tb", 32), ("k16", 32),
-               ("kw", 2 * C), ("ki", HALF), ("wb", 2 * C), ("so", 2 * C), ("cnt", C), ("pf", 64), ("pt", 64),
-               ("pu", 64), ("pw", 64), ("df", 44), ("e0", C), ("e1", C), ("eg0", C), ("eg1", C), ("sc0", C),
-               ("sc1", C), ("r0", C), ("r1", C), ("wd", C), ("wg", C), ("sg", C), ("tg", 24), ("lf", 2 * C), ("yb", C)):
+               ("kw", 2 * C), ("ki", C), ("wd", C), ("wb", 2 * C), ("so", 2 * C), ("cnt", C), ("df", 44), ("e0", C),
+               ("e1", C), ("eg0", C), ("eg1", C), ("sc0", C), ("sc1", C), ("r0", C), ("r1", C), ("wg", C), ("sg", C),
+               ("tg", 22), ("lf", 2 * C), ("yb", C)):
     SCRATCH[_n] = ("sbuf", [128, _w], F32)
-SCRATCH["pi"] = ("sbuf", [128, 44], I32)
-for _n, _w in (("o16", 38), ("p16", 44), ("l0", 24), ("l0c", 22), ("l1", 22), ("n0", 24), ("n1", 24), ("q16", 22)):
+for _n in ("pi", "pj"):
+    SCRATCH[_n] = ("sbuf", [128, 44], I32)
+for _n, _w in (("o16", 38), ("p16", 44), ("l0", 24), ("l1", 24), ("n0", 24), ("n1", 24), ("q16", 22)):
     SCRATCH[_n] = ("sbuf", [128, _w], U16)
 for _n, _w in (("u", 128), ("up", 256), ("v", 128), ("w", 512), ("z", 512), ("e", 512), ("s0", C), ("o0", HALF),
                ("m0", C), ("o1", HALF), ("s1", C), ("m1", C), ("h1", C), ("s2", C), ("o2", HALF), ("s3", C),
@@ -28,8 +45,8 @@ for _n, _w in (("u", 128), ("up", 256), ("v", 128), ("w", 512), ("z", 512), ("e"
 for _k in range(8):
     SCRATCH["ps%d" % _k] = ("psum", [128, 512], F32)
 
-SEMAPHORES = (["kv", "ka", "kp", "kg", "go"] + ["arr%d" % k for k in range(4)] + ["left%d" % k for k in range(4)]
-              + ["d%d" % k for k in range(12)] + ["outs", "outa"])
+SEMAPHORES = (["kv", "ka", "kp", "kg", "go", "arrc"] + ["arr%d" % k for k in range(4)]
+              + ["left%d" % k for k in range(4)] + ["d%d" % k for k in range(16)] + ["outs", "outa"])
 
 
 def _flat(x, out):
@@ -49,353 +66,299 @@ def rank_program(g, core, T, topo):
     queue = {"v": g.vector, "a": g.scalar, "p": g.tensor, "g": g, "s": g.sync}
     ops = []
 
-    def op(eng, fn, *deps):
-        o = {"eng": eng, "fn": fn, "deps": _flat(deps, []), "sem": "k" + eng, "kind": "c", "used": False}
+    def op(name, eng, fn, *deps):
+        o = {"name": name, "eng": eng, "fn": fn, "deps": _flat(deps, []), "sem": "k" + eng, "kind": "c", "used": False}
         ops.append(o)
         return o
 
     dmas = [0]
 
-    def dma(eng, out, in_, *deps, sem=None):
+    def dma(name, eng, out, in_, *deps, sem=None):
         if sem is None:
             sem = "d%d" % dmas[0]
             dmas[0] += 1
-        o = op(eng, lambda q: q.dma_start(out, in_), *deps)
+        o = op(name, eng, lambda q: q.dma_start(out, in_), *deps)
         o.update(sem=sem, kind="d", used=True)
         return o
 
-    def event(sem, val):
-        return {"sem": sem, "val": val, "clock": {sem: val}, "kind": "e", "used": True}
+    def event(sem, val, src):
+        return {"sem": sem, "val": val, "clock": {sem: val}, "kind": "e", "used": True, "src": src}
 
     def pair(name, a, b):
         return T["c_" + name][:, a:b], T["s_" + name][:, a:b]
 
-    def quant(name, a, n, tile, *deps):
-        c, s = pair(name, a, a + n)
-        return op("v", lambda q: q.quantize_mx(c, s, tile), *deps)
+    def half(name, h):
+        return pair(name, HALF * h, HALF * h + HALF)
 
-    free = [None] * 8
+    def quant(name, dst, tile, *deps):
+        return op(name, "v", lambda q: q.quantize_mx(dst[0], dst[1], tile), *deps)
 
-    def mm(bank, lhs, rhs, n, *deps):
-        out = T["ps%d" % bank][:, 0:n]
-        return op("p", lambda q: q.matmul_mx(out, lhs[0], lhs[1], rhs[0], rhs[1], True, True), free[bank], *deps)
+    last = [None] * 8
 
-    def evac(eng, bank, n, out, scale, relu, dep):
-        src = T["ps%d" % bank][:, 0:n]
-        if eng == "a":
-            f = ACT.Relu if relu else ACT.Copy
-            o = op("a", lambda q: q.activation(out, src, f, scale=scale), dep)
-        elif relu:
-            o = op("v", lambda q: q.tensor_scalar(out, src, 0.0, scale, ALU.max, ALU.mult), dep)
-        elif scale == 1.0:
-            o = op("v", lambda q: q.tensor_copy(out, src), dep)
-        else:
-            o = op("v", lambda q: q.tensor_scalar(out, src, scale, None, ALU.mult), dep)
-        free[bank] = o
+    def banked(o, bank):
+        if last[bank] is not None:
+            o["deps"].append(last[bank])
+        last[bank] = o
         return o
 
-    def copy(eng, out, in_, *deps):
+    def mm(name, bank, lhs, rhs, *deps):
+        out = T["ps%d" % bank][:, 0:HALF]
+        return banked(op(name, "p", lambda q: q.matmul_mx(out, lhs[0], lhs[1], rhs[0], rhs[1], True, True), *deps), bank)
+
+    def evac(name, eng, bank, out, scale=1.0, relu=False):
+        src = T["ps%d" % bank][:, 0:HALF]
         if eng == "a":
-            return op("a", lambda q: q.activation(out, in_, ACT.Copy), *deps)
-        return op("v", lambda q: q.tensor_copy(out, in_), *deps)
+            f = ACT.Relu if relu else ACT.Copy
+            o = op(name, "a", lambda q: q.activation(out, src, f, scale=scale))
+        elif relu:
+            o = op(name, "v", lambda q: q.tensor_scalar(out, src, 0.0, scale, ALU.max, ALU.mult))
+        elif scale == 1.0:
+            o = op(name, "v", lambda q: q.tensor_copy(out, src))
+        else:
+            o = op(name, "v", lambda q: q.tensor_scalar(out, src, scale, None, ALU.mult))
+        return banked(o, bank)
 
-    def ts(out, in0, s1, s2, o0, o1, *deps):
+    def copy(name, eng, out, in_, *deps):
+        if eng == "g":
+            return op(name, "g", lambda q: q.affine_select(out, in_, [[0, HALF]], ALU.is_ge, 0.0, 0, 0), *deps)
+        if eng == "a":
+            return op(name, "a", lambda q: q.activation(out, in_, ACT.Copy), *deps)
+        return op(name, "v", lambda q: q.tensor_copy(out, in_), *deps)
+
+    def times(name, out, in_, scale, *deps):
+        return op(name, "a", lambda q: q.activation(out, in_, ACT.Copy, scale=scale), *deps)
+
+    def ts(name, out, in0, s1, s2, o0, o1, *deps):
         if o1 is None:
-            return op("v", lambda q: q.tensor_scalar(out, in0, s1, None, o0), *deps)
-        return op("v", lambda q: q.tensor_scalar(out, in0, s1, s2, o0, o1), *deps)
+            return op(name, "v", lambda q: q.tensor_scalar(out, in0, s1, None, o0), *deps)
+        return op(name, "v", lambda q: q.tensor_scalar(out, in0, s1, s2, o0, o1), *deps)
 
-    def tt(out, in0, in1, o, *deps):
-        return op("v", lambda q: q.tensor_tensor(out, in0, in1, o), *deps)
+    def tt(name, out, in0, in1, o, *deps):
+        return op(name, "v", lambda q: q.tensor_tensor(out, in0, in1, o), *deps)
 
-    def scan(out, k, x, *deps):
-        return op("v", lambda q: q.tensor_tensor_scan(out, k, x, 0.0, ALU.mult, ALU.add), *deps)
+    def scan(name, out, k, x, *deps):
+        return op(name, "v", lambda q: q.tensor_tensor_scan(out, k, x, 0.0, ALU.mult, ALU.add), *deps)
 
-    def iota(out, pattern, base, cm):
-        return op("g", lambda q: q.iota(out, pattern, base, cm, allow_small_or_imprecise_dtypes=True))
+    def fill(name, ap):
+        return op(name, "v", lambda q: q.memset(ap, 0.0))
+
+    def iota(name, out, pattern, base, cm, *deps):
+        return op(name, "g", lambda q: q.iota(out, pattern, base, cm, allow_small_or_imprecise_dtypes=True), *deps)
 
     def send(k, src, dst, t, dep):
         d = FAR[t]
         peer = T.cores[rank + d if (rank // d) % 2 == 0 else rank - d]
         rid, pid = topo.addr(peer, core)
         mask = topo.mask(core, peer)
-        n = 2 * len(topo.engines(core, peer))
-        sc, ss = pair(src, 0, HALF)
-        dc, ds = pair(dst, HALF, C)
+        n = len(topo.engines(core, peer))
+        (sc, ss), (dc, ds) = half(src, 0), half(dst, 1)
         arr, left = T.sem["arr%d" % k], T.sem["left%d" % k]
-        a = op("g", lambda q: q.remote_dma(dc.bitcast(dt.uint8), sc.bitcast(dt.uint8), arr, left, pid, rid, mask), dep)
-        b = op("g", lambda q: q.remote_dma(ds, ss, arr, left, pid, rid, mask))
+        arrc = T.sem.arrc if k == 3 else arr
+        a = op("sc%d" % k, "g", lambda q: q.remote_dma(dc.bitcast(dt.uint8), sc.bitcast(dt.uint8), arrc, left, pid, rid,
+                                                       mask), dep)
+        b = op("ss%d" % k, "g", lambda q: q.remote_dma(ds, ss, arr, left, pid, rid, mask))
         a["kind"] = b["kind"] = "r"
-        return event("arr%d" % k, n), event("left%d" % k, n)
+        b["deps"].append(a)
+        if k == 3:
+            return [event("arrc", n, a), event("arr3", n, b)], event("left3", 2 * n, b)
+        return event("arr%d" % k, 2 * n, b), event("left%d" % k, 2 * n, b)
 
     W = [pair("w", 128 * b, 128 * b + 128) for b in range(4)]
     Z = [pair("z", 128 * b, 128 * b + 128) for b in range(4)]
     E = [pair("e", 128 * b, 128 * b + 128) for b in range(4)]
     U = [pair("up", 128 * t, 128 * t + 128) for t in range(2)]
 
-    l_xu = dma("s", T.xt[:, 4 * HALF:4 * C], T.x[:, 4 * HALF:4 * C])
-    o = op("s", lambda q: q.sem_inc(T.sem.go, 1))
-    o["kind"] = "r"
-    l_p0 = dma("s", T.pi[:, 0:22], T.p0[:])
-    l_xl = dma("s", T.xt[:, 0:4 * HALF], T.x[:, 0:4 * HALF])
-    l_p1 = dma("a", T.pi[:, 22:44], T.p1[:], event("go", 1))
-    l_u = dma("a", T.ut[:], T.u[:])
+    l_xu = dma("lxu", "s", T.xt[:, 4 * HALF:4 * C], T.x[:, 4 * HALF:4 * C])
+    go = op("go", "s", lambda q: q.sem_inc(T.sem.go, 1), {"kind": "r", "src": l_xu})
+    go["kind"] = "r"
+    l_p0 = dma("lp0", "s", T.pi[:, 0:22], T.p0[:], go)
+    l_xl = dma("lxl", "s", T.xt[:, 0:4 * HALF], T.x[:, 0:4 * HALF], go)
+    l_p1 = dma("lp1", "a", T.pi[:, 22:44], T.p1[:], event("go", 1, go))
+    l_u = dma("lu", "a", T.ut[:], T.u[:], event("go", 1, go))
 
-    i_a = iota(T.xi[:, 0:32], [[0, 2], [2, 8], [0, 2]], 1, 0)
-    i_b = iota(T.xi[:, 32:64], [[0, 2], [1, 16]], 0, 0)
-    i_u = iota(T.xo[:, 64:80], [[1, 2], [16, 8]], 0, 0)
-    i_v = iota(T.iv[:, 0:130], [[1, 130]], -1, 0)
-    i_p = iota(T.pcol[:, 0:1], [[0, 1]], 0, 1)
+    i_a = iota("ia", T.xi[:, 0:32], [[0, 2], [2, 8], [0, 2]], 1, 0)
+    i_b = iota("ib", T.xi[:, 32:64], [[0, 2], [1, 16]], 0, 0)
+    i_v = iota("iv", T.iv[:, 0:130], [[1, 130]], -1, 0)
+    i_p = iota("ip", T.pcol[:, 0:1], [[0, 1]], 0, 1)
+    i_u = iota("iu", T.xo[:, 64:80], [[1, 2], [16, 8]], 0, 0)
 
-    m_z0 = op("v", lambda q: q.memset(T.z0[:], 0.0))
-    m_z1 = op("v", lambda q: q.memset(T.z1[:], 0.0))
-    m_pf = op("v", lambda q: q.memset(T.pf[:, 44:64], 0.0))
-    t_x = op("v", lambda q: q.transpose(T.xo[:, 0:64], T.xi[:]), i_b)
-    m_wb = op("v", lambda q: q.memset(T.wb[:, 1:2 * C:2], 0.0))
+    q_xu = quant("qxu", half("o0", 0), T.xt[:, 4 * HALF:4 * C], l_xu)
+    arr0, left0 = send(0, "o0", "s0", 0, q_xu)
+
+    m_z0, m_z1 = fill("mz0", T.z0[:]), fill("mz1", T.z1[:])
+    m_wb = iota("mwb", T.wb[:, 1:2 * C:2], [[0, C]], 0, 0, left0["src"])
+    t_x = op("tx", "v", lambda q: q.transpose(T.xo[:, 0:64], T.xi[:]), i_a, i_b)
     s1, pm = T.xo[:, 31:32], T.xo[:, 32:33]
-    c_o = copy("v", T.o16[:], T.xo[:, 42:80], t_x, i_u)
-    ts(T.ta[:, 0:16], T.iv[:, 1:17], s1, BIG, ALU.is_equal, ALU.mult, t_x, i_v)
-    ts(T.tb[:, 0:16], T.iv[:, 2:18], s1, None, ALU.not_equal, None)
-    ts(T.ta[:, 16:32], T.iv[:, 0:16], pm, BIG, ALU.is_equal, ALU.mult)
-    k4 = ts(T.tb[:, 16:32], T.iv[:, 1:17], pm, None, ALU.not_equal, None)
-    c_c = ts(T.cc[:, 0:2], T.xo[:, 31:33], 15.0, 1.0 / BIG, ALU.is_equal, ALU.max)
-    k16 = tt(T.k16[:], T.ta[:], T.tb[:], ALU.max, k4)
+    c_o = copy("co", "v", T.o16[:], T.xo[:, 42:80], t_x, i_u)
+    k1 = ts("k1", T.ta[:, 0:16], T.iv[:, 1:17], s1, BIG, ALU.is_equal, ALU.mult, t_x, i_v)
+    k2 = ts("k2", T.tb[:, 0:16], T.iv[:, 2:18], s1, None, ALU.not_equal, None, t_x, i_v)
+    k3 = ts("k3", T.ta[:, 16:32], T.iv[:, 0:16], pm, BIG, ALU.is_equal, ALU.mult, t_x, i_v)
+    k4 = ts("k4", T.tb[:, 16:32], T.iv[:, 1:17], pm, None, ALU.not_equal, None, t_x, i_v)
+    c_c = ts("cc", T.cc[:, 0:2], T.xo[:, 31:33], 15.0, 1.0 / BIG, ALU.is_equal, ALU.max, t_x)
+    k16 = tt("k16", T.k16[:], T.ta[:], T.tb[:], ALU.max, k1, k2, k3, k4)
     cw, ci = T.cc[:, 0:1], T.cc[:, 1:2]
-    e1 = ts(T.z0[:, 2:514:4], T.iv[:, 1:129], T.pcol[:, 0:1], 0.5, ALU.is_equal, ALU.mult, i_p, m_z0)
-    e2 = ts(T.z1[:, 3:515:4], T.iv[:, 1:129], T.pcol[:, 0:1], 0.5, ALU.is_equal, ALU.mult, m_z1)
-    q_e = []
-    for b in range(5):
-        if b == NPRE:
-            q_xu = quant("o0", 0, HALF, T.xt[:, 4 * HALF:4 * C], l_xu)
-            arr0, left0 = send(0, "o0", "s0", 0, q_xu)
-        if b < 4:
-            a = 2 - 2 * (b // 2)
-            q_e.append(quant("e", 128 * b, 128, (T.z0, T.z1)[b % 2][:, a:a + 512], e1, e2))
+    e1 = ts("e1", T.z0[:, 2:514:4], T.iv[:, 1:129], T.pcol[:, 0:1], 0.5, ALU.is_equal, ALU.mult, i_v, i_p, m_z0)
+    e2 = ts("e2", T.z1[:, 3:515:4], T.iv[:, 1:129], T.pcol[:, 0:1], 0.5, ALU.is_equal, ALU.mult, i_v, i_p, m_z1)
+    q_e = [quant("qe%d" % b, E[b], (T.z0, T.z1)[b % 2][:, 2 - 2 * (b // 2):514 - 2 * (b // 2)], (e1, e2)[b % 2])
+           for b in range(4)]
     cnt = []
     for a, n in ((0, 128), (128, 128), (256, 96)):
-        cnt.append(op("a", lambda q, a=a, n=n: q.activation(T.cnt[:, a:a + n], T.iv[:, 1:1 + n], ACT.Identity,
-                                                           bias=float(512 + a)), i_v))
-    kw0 = copy("a", T.kw[:, 0:C], T.k16[:, 0:16].indirect(T.o16[:, 0:22]), k16, c_o)
-    ki = copy("a", T.ki[:], T.k16[:, 16:32].indirect(T.o16[:, 0:11]))
-    kw1 = copy("a", T.kw[:, C:2 * C], T.kw[:, 0:C], kw0)
-    p_f = copy("v", T.pf[:, 0:44], T.pi[:], l_p0, l_p1, m_pf)
-    p16 = copy("v", T.p16[:], T.pi[:])
-    p_t = op("v", lambda q: q.transpose(T.pt[:], T.pf[:]), p_f)
-    copy("v", T.pu[:, 0:64:2], T.pt[:, 1:64:2], p_t)
-    w_b = copy("v", T.pu[:, 1:64:2], T.pt[:, 0:64:2])
-    q_xl = quant("s0", 0, HALF, T.xt[:, 0:4 * HALF], l_xl)
-    p_w = op("v", lambda q: q.transpose(T.pw[:], T.pu[:]), w_b)
-    q_u = quant("u", 0, 128, T.ut[:], l_u)
-    p_d = tt(T.df[:], T.pw[:, 0:44], T.pf[:, 0:44], ALU.subtract, p_w)
+        cnt.append(op("cnt%d" % a, "a", lambda q, a=a, n=n: q.activation(
+            T.cnt[:, a:a + n], T.iv[:, 1:1 + n], ACT.Identity, bias=float(512 + a)), i_v))
+    kw0 = copy("kw0", "a", T.kw[:, 0:C], T.k16[:, 0:16].indirect(T.o16[:, 0:22]), k16, c_o)
+    ki = copy("ki", "a", T.ki[:], T.k16[:, 16:32].indirect(T.o16[:, 0:22]), k16, c_o)
+    kw1 = copy("kw1", "a", T.kw[:, C:2 * C], T.kw[:, 0:C], kw0)
+    l_pj = [dma("lj%d%d" % (t, k), "sa"[t], T.pj[k:128:2, 22 * t:22 * t + 22], (T.p0, T.p1)[t][1 - k:128:2, :],
+                (go, event("go", 1, go))[t]) for t in range(2) for k in range(2)]
+    p16 = copy("p16", "v", T.p16[:], T.pi[:], l_p0, l_p1)
+    p_d = tt("pd", T.df[:], T.pj[:], T.pi[:], ALU.subtract, l_pj, l_p0, l_p1)
+    kslot = times("kslot", T.kw[:, 15:2 * C:16], T.df[:], cw, p_d, kw1, c_c)
+    wslot = copy("wslot", "v", T.wb[:, 15:2 * C:16], T.pi[:], l_p0, l_p1, m_wb)
+
+    q_xl = quant("qxl", half("s0", 0), T.xt[:, 0:4 * HALF], l_xl)
+    q_u = quant("qu", pair("u", 0, 128), T.ut[:], l_u)
     uo = T.o16[:, 22:38]
-    pk_c = op("v", lambda q: q.tensor_copy(T.c_up[:].bitcast(dt.uint32), T.c_u[:].bitcast(dt.uint32).indirect(uo)),
-              q_u, c_o)
-    kslot = ts(T.kw[:, 15:2 * C:16], T.df[:], cw, None, ALU.mult, None, p_d, kw1, c_c)
-    wslot = copy("a", T.wb[:, 15:2 * C:16], T.pf[:, 0:44], p_f, m_wb)
+    pk = [op("pkc", "v", lambda q: q.tensor_copy(T.c_up[:].bitcast(dt.uint32),
+                                                 T.c_u[:].bitcast(dt.uint32).indirect(uo)), q_u, c_o),
+          copy("pks", "a", T.s_up[:], T.s_u[:].indirect(uo), q_u, c_o)]
+    sct1 = copy("sct1", "v", T.sc1[:].indirect(T.p16[:, 22:34]), T.cnt[:, 0:192], p16, cnt)
+    sct1 = copy("sct2", "v", T.sc1[:].indirect(T.p16[:, 34:44]), T.cnt[:, 192:C], sct1)
+    r1 = scan("r1", T.r1[:], T.ki[:], T.sc1[:], sct1, ki)
+    q16 = ts("q16", T.q16[:], T.r1[:, 15:C:16], ci, -512.0, ALU.mult, ALU.add, r1, c_c)
 
-    def whole(t, b):
-        return t == 0 or b >= HY[t]
+    l_ws = dma("lws", "s", T.s_w[:], T.ws[:], left0)
+    l_wc = dma("lwc", "s", T.c_w[:].bitcast(dt.uint8), T.wc[:], left0)
 
-    def unpack(t, S, banks, dep):
-        rhs = pair(S, HALF, C)
-        sc = mm(banks[0], U[t], rhs, HALF, dep)
-        return sc, [mm(banks[1 + b], E[b], pair(S, 0, C), C) if whole(t, b) else mm(banks[1 + b], E[b], rhs, HALF)
-                    for b in range(4)]
+    ev, dv, at = {}, {}, {}
 
-    def number(eng, name, t, a, b, banks, mms):
-        lo = a if whole(t, b) else 0
-        o = copy(eng, T[name % t][:, C * b + a:C * b + a + HALF], T["ps%d" % banks[1 + b]][:, lo:lo + HALF], mms[b])
-        free[banks[1 + b]] = o
-        return o
+    def unpack(t, h, S, sb, banks, dep):
+        a = HALF * h
+        mm("se%d%d" % (t, h), sb, U[t], half(S, h), dep, pk)
+        ev[t, h] = evac("e%d%d" % (t, h), PLAN["e"][2 * t + h], sb, T["e%d" % t][:, a:a + HALF])
+        for b in range(4):
+            mm("sd%d%d%d" % (t, h, b), banks[b], E[b], half(S, h), dep, q_e[b])
+            dv[t, h, b] = evac("d%d%d%d" % (t, h, b), PLAN["d%d%d" % (t, h)][b], banks[b],
+                               T["dh%d" % t][:, C * b + a:C * b + a + HALF])
+            at[t, h, b] = banks[b]
 
-    def upper(plan, t, banks, mms, more):
-        d, c, x = [None] * 4, [None] * 4, None
-        for w in plan.split():
-            if w == "g":
-                x = more()
-            elif w[0] == "d":
-                d[int(w[1])] = number("a", "dh%d", t, HALF, int(w[1]), banks, mms)
+    def lst(name, h):
+        return T[name][:, 12 * h:12 * h + 11]
+
+    def lists(t, first):
+        e, eg, out, done = T["e%d" % t], T["eg%d" % t], [None, None], []
+        cut = ((0, 6), (6, 12), (12, 22)) if first == 0 else ((10, 16), (16, 22), (0, 10))
+        ga = [copy("ga%d%d" % (t, k), PLAN["ga"][3 * t + k], eg[:, 16 * c0:16 * c1],
+                   e[:].indirect(T.p16[:, 22 * t + c0:22 * t + c1]), ev[t, 0], ev[t, 1], p16)
+              for k, (c0, c1) in enumerate(cut)]
+        for h, (c0, c1), got in ((first, (cut[0][0], cut[1][1]), ga[:2]), (1 - first, cut[2], ga[2])):
+            done.append(tt("w%d%d" % (t, h), T.wb[:, C * t + 16 * c0:C * t + 16 * c1:2], eg[:, 16 * c0 + 1:16 * c1:2],
+                           eg[:, 16 * c0:16 * c1:2], ALU.is_gt, got))
+            a = C * t + HALF * h
+            sc = scan("sn%d%d" % (t, h), T.so[:, a:a + HALF], T.kw[:, a:a + HALF], T.wb[:, a:a + HALF], done,
+                      kslot, wslot)
+            out[h] = copy("l%d%d" % (t, h), "v", lst("l%d" % t, h), T.so[:, a + 15:a + HALF:16], sc)
+        return out, done
+
+    def mix(t, h, dst, l):
+        a, off, dh, done = HALF * h, lst("l%d" % t, h), T["dh%d" % t], []
+        for b in range(4):
+            out, win, name = T["mp%d" % t][:, 4 * a + b:4 * (a + HALF):4], dh[:, C * b:C * b + C], "%d%d%d" % (t, h, b)
+            if PLAN["m%d%d" % (t, h)][b] == "f":
+                dc = T["dc%d" % t][:, C * b + a:C * b + a + HALF]
+                c = copy("c" + name, PLAN["c%d%d" % (t, h)][b], dc, dh[:, C * b + a:C * b + a + HALF], dv[t, h, b])
+                done.append(tt("m" + name, out, win.indirect(off), dc, ALU.add, l, c, dv[t, 0, b], dv[t, 1, b]))
             else:
-                c[int(w[1])] = number("a", "dc%d", t, HALF, int(w[1]), banks, mms)
-        return d, c, x
+                tm = T["tm%d" % t][:, C * b + a:C * b + a + HALF]
+                got = copy("t" + name, "a", tm, win.indirect(off), l, dv[t, 0, b], dv[t, 1, b])
+                done.append(banked(tt("m" + name, out, tm, T["ps%d" % at[t, h, b]][:, 0:HALF], ALU.add, got),
+                                   at[t, h, b]))
+        return quant("qp%d%d" % (t, h), dst, T["mp%d" % t][:, 4 * a:4 * (a + HALF)], done)
 
-    bk = [0, 1, 2, 3, 4]
-    dm = [mm(bk[1 + b], E[b], pair("s0", 0, HALF), HALF, q_xl, q_e) for b in range(4)]
-    d0l = [number("a", "dh%d", 0, 0, b, bk, dm) for b in range(2)]
-    pk_s = copy("a", T.s_up[:], T.s_u[:].indirect(uo), q_u, c_o)
-    d0l += [number("a", "dh%d", 0, 0, b, bk, dm) for b in range(2, 4)]
-    e0l = evac("a", bk[0], HALF, T.e0[:, 0:HALF], 1.0, False, mm(bk[0], U[0], pair("s0", 0, HALF), HALF, pk_c, pk_s))
-    sct1 = copy("v", T.sc1[:].indirect(T.p16[:, 22:44]), T.cnt[:], p16, cnt)
+    def forward(t, h, src, dst, banks, *deps):
+        a, H, done = HALF * h, T["mh%d" % t], []
+        for b in range(4):
+            mm("sw%d%d%d" % (t, h, b), banks[b], W[b], half(src, h), *deps)
+            done.append(evac("h%d%d%d" % (t, h, b), PLAN["h%d%d" % (t, h)][b], banks[b],
+                             H[:, 4 * a + b:4 * (a + HALF):4], 0.03125, True))
+        return quant("qh%d%d" % (t, h), half(dst, h), H[:, 4 * a:4 * (a + HALF)], done)
 
-    l_ws = dma("s", T.s_w[:], T.ws[:], left0)
-    l_wc = dma("s", T.c_w[:].bitcast(dt.uint8), T.wc[:])
+    gv = {}
 
-    def switch(t, eg, a, b, dep):
-        return tt(T.wb[:, C * t + a:C * t + b:2], eg[:, a + 1:b:2], eg[:, a:b:2], ALU.is_gt, dep, wslot)
+    def backward(t, h, src, banks, *deps):
+        a = HALF * h
+        for b in range(4):
+            mm("sz%d%d%d" % (t, h, b), banks[b], Z[b], half(src, h), *deps)
+            gv[t, h, b] = evac("g%d%d%d" % (t, h, b), PLAN["g%d%d" % (t, h)][b], banks[b],
+                               T["mg%d" % t][:, C * b + a:C * b + a + HALF], 0.03125)
 
-    def places(t, a, b, dep):
-        a, b = C * t + a, C * t + b
-        return scan(T.so[:, a:b], T.kw[:, a:b], T.wb[:, a:b], dep, kslot)
+    def undo(t, h, dst, n):
+        a, X, G = HALF * h, T["mx%d" % t], T["mg%d" % t]
+        done = [copy("x%d%d%d" % (t, h, b), PLAN["x%d%d" % (t, h)][b], X[:, 4 * a + b:4 * (a + HALF):4],
+                     G[:, C * b:C * b + C].indirect(lst("n%d" % t, h)), n, gv[t, 0, b], gv[t, 1, b]) for b in range(4)]
+        return quant("qx%d%d" % (t, h), dst, X[:, 4 * a:4 * (a + HALF)], done)
 
-    def fetch(t, h, off, a, n, dep, *per):
-        return [None] * h + [copy("a", T["tm%d" % t][:, C * b + a:C * b + a + n],
-                                  T["dh%d" % t][:, C * b:C * b + C].indirect(off), dep, [d[b] for d in per])
-                             for b in range(h, 4)]
+    LO, HI = (0, 1, 2, 3), (5, 6, 7, 4)
+    unpack(0, 0, "s0", 4, LO, q_xl)
+    unpack(0, 1, "s0", 4, (5, 6, 7, 0), arr0)
+    l0, w0 = lists(0, 1)
+    arr1, left1 = send(1, "o1", "m0", 1, mix(0, 1, half("o1", 0), l0[1]))
+    q_pl = mix(0, 0, half("m0", 0), l0[0])
+    l_zs = dma("lzs", "s", T.s_z[:], T.zs[:], left1)
+    l_zc = dma("lzc", "s", T.c_z[:].bitcast(dt.uint8), T.zc[:], left1)
+    l_v = dma("lv", "s", T.vt[:], T.v[:], left1)
+    unpack(1, 0, "s1", 4, LO, forward(0, 0, "m0", "s1", (4, 5, 6, 7), q_pl, l_ws, l_wc))
+    unpack(1, 1, "s1", 0, HI, forward(0, 1, "m0", "s1", HI, arr1, l_ws, l_wc))
 
-    def mix(t, off, a, n, b, banks, got, *deps):
-        out = T["mp%d" % t][:, 4 * a + b:4 * (a + n):4]
-        if got[b] is None:
-            return tt(out, T["dh%d" % t][:, C * b:C * b + C].indirect(off), T["dc%d" % t][:, C * b + a:C * b + a + n],
-                      ALU.add, *deps)
-        o = tt(out, T["tm%d" % t][:, C * b + a:C * b + a + n], T["ps%d" % banks[1 + b]][:, a:a + n], ALU.add, got[b])
-        free[banks[1 + b]] = o
-        return o
+    fst = PLAN["first"]
+    l1, w1 = lists(1, fst)
+    q_p = {h: mix(1, h, half("m1", h), l1[h]) for h in (fst, 1 - fst)}
+    q_h = {h: forward(1, h, "m1", "h1", (LO, HI)[h], q_p[h]) for h in (fst, 1 - fst)}
+    for h in (fst, 1 - fst):
+        backward(1, h, "h1", (LO, HI)[h], q_h[h], l_zs, l_zc)
+    wd = [copy("wd0", PLAN["wd"], T.wd[:, 0:C:2], T.wb[:, C:2 * C:2], w1),
+          times("wd1", T.wd[:, 1:C:2], T.wb[:, C:2 * C:2], -1.0, w1)]
+    wg = [copy("wg0", PLAN["wg"][0], T.wg[:, 0:160], T.wd[:].indirect(T.q16[:, 0:10]), wd, q16),
+          copy("wg1", PLAN["wg"][1], T.wg[:, 160:C], T.wd[:].indirect(T.q16[:, 10:22]), wd, q16)]
 
-    bk = [5, 6, 7, 0, 1]
-    sc, dm = unpack(0, "s0", bk, arr0)
-    e0u = evac("v", bk[0], HALF, T.e0[:, HALF:C], 1.0, False, sc)
-    d0u, c0u, gb = upper("d0 g d1 d2 d3", 0, bk, dm, lambda: copy(
-        "a", T.eg0[:, 0:160], T.e0[:].indirect(T.p16[:, 0:10]), e0u, e0l, p16))
-    ga = copy("v", T.eg0[:, 160:C], T.e0[:].indirect(T.p16[:, 10:22]), e0u, e0l, p16)
-    c0u[0] = copy("v", T.dc0[:, HALF:C], T.dh0[:, HALF:C], d0u[0])
-    wa = switch(0, T.eg0, 160, C, ga)
-    wl = switch(0, T.eg0, 0, 160, gb)
-    sa = places(0, 160, C, wa)
-    c0u[1] = copy("v", T.dc0[:, C + HALF:2 * C], T.dh0[:, C + HALF:2 * C], d0u[1])
-    l0u = copy("v", T.l0[:, 12:23], T.so[:, HALF + 15:C:16], sa)
-    sl = places(0, 0, 160, wl)
-    got = fetch(0, HY[0], T.l0[:, 12:23], HALF, HALF, l0u, d0u, d0l)
-    mu = [mix(0, T.l0[:, 12:23], HALF, HALF, 0, bk, got, l0u, d0u[0], c0u[0], d0l[0])]
-    l0l = copy("v", T.l0[:, 0:11], T.so[:, 15:HALF:16], sl)
-    mu += [mix(0, T.l0[:, 12:23], HALF, HALF, b, bk, got, l0u, d0u[b], c0u[b], d0l[b]) for b in range(1, 4)]
-    q_pu = quant("o1", 0, HALF, T.mp0[:, 4 * HALF:4 * C], mu)
-    arr1, left1 = send(1, "o1", "m0", 1, q_pu)
-    got = fetch(0, 0, T.l0[:, 0:11], 0, HALF, l0l)
-    ml = [mix(0, T.l0[:, 0:11], 0, HALF, b, bk, got, l0l) for b in range(4)]
-    q_pl = quant("m0", 0, HALF, T.mp0[:, 0:4 * HALF], ml)
+    def inverse1(h):
+        a, c = HALF * h, slice(11 * h, 11 * h + 11)
+        s = scan("sg%d" % h, T.sg[:, a:a + HALF], T.ki[:, 0:HALF], T.wg[:, a:a + HALF], wg[h:])
+        s = tt("tg%d" % h, T.tg[:, c], T.sg[:, a + 15:a + HALF:16], T.r1[:, a + 15:a + HALF:16], ALU.add, s)
+        return ts("n1%d" % h, lst("n1", h), T.tg[:, c], ci, -512.0, ALU.mult, ALU.add, s)
 
-    l_zs = dma("s", T.s_z[:], T.zs[:], left1)
-    l_zc = dma("s", T.c_z[:].bitcast(dt.uint8), T.zc[:])
-    l_v = dma("s", T.vt[:], T.v[:])
+    arr2, left2 = send(2, "o2", "s2", 1, undo(1, 1, half("o2", 0), inverse1(1)))
 
-    def layer(M, src, a, n, banks, *deps):
-        rhs = pair(src, a, a + n)
-        return [mm(banks[b], M[b], rhs, n, *deps) for b in range(4)]
-
-    def relu(eng, H, a, n, b, banks, mms):
-        return evac(eng, banks[b], n, H[:, 4 * a + b:4 * (a + n):4], 0.03125, True, mms[b])
-
-    def plain(eng, G, a, n, b, banks, mms):
-        return evac(eng, banks[b], n, G[:, C * b + a:C * b + a + n], 0.03125, False, mms[b])
-
-    bk = [2, 3, 4, 5]
-    mms = layer(W, "m0", 0, HALF, bk, q_pl, l_ws, l_wc)
-    scan(T.r1[:, 0:HALF], T.ki[:], T.sc1[:, 0:HALF], sct1, ki)
-    r1b = scan(T.r1[:, HALF:C], T.ki[:], T.sc1[:, HALF:C])
-    hs = [relu("av"[b % 2], T.mh0, 0, HALF, b, bk, mms) for b in range(4)]
-    q_hl = quant("s1", 0, HALF, T.mh0[:, 0:4 * HALF], hs)
-    bk, bu = [6, 7, 0, 1, 2], [3, 4, 5, 6]
-    rhs = pair("s1", 0, HALF)
-    l0c = copy("v", T.l0c[:], T.so[:, 15:C:16], sl)
-    q16 = ts(T.q16[:], T.r1[:, 15:C:16], ci, -512.0, ALU.mult, ALU.add, r1b)
-    dm = [mm(bk[1 + b], E[b], rhs, HALF, q_hl) for b in range(3)]
-    d1l = [number("ava"[b], "dh%d", 1, 0, b, bk, dm) for b in range(3)]
-    mms = layer(W, "m0", HALF, HALF, bu, arr1)
-    hs = [relu("av"[b % 2], T.mh0, HALF, HALF, b, bu, mms) for b in range(4)]
-    dm.append(mm(bk[4], E[3], rhs, HALF))
-    e1l = evac("a", 3, HALF, T.e1[:, 0:HALF], 1.0, False, mm(3, U[1], rhs, HALF))
-    d1l.append(number("a", "dh%d", 1, 0, 3, bk, dm))
-    q_hu = quant("s1", HALF, HALF, T.mh0[:, 4 * HALF:4 * C], hs)
-
-    NB, KA = C - NA, NA // 16
-    bk = [7, 0, 1, 2, 3]
-    sc, dm = unpack(1, "s1", bk, q_hu)
-    c1l = [copy("v", T.dc1[:, C * b:C * b + HALF], T.dh1[:, C * b:C * b + HALF], d1l[b]) for b in range(HY[1])]
-    c1l += [None] * 4
-    e1u = evac("v", bk[0], HALF, T.e1[:, HALF:C], 1.0, False, sc)
-    d1u, c1u, gb = upper("d0 g c0 d1 c1 d2 d3 c2", 1, bk, dm, lambda: copy(
-        "a", T.eg1[:, NA:C], T.e1[:].indirect(T.p16[:, 22 + KA:44]), e1u, e1l))
-    ga = copy("v", T.eg1[:, 0:NA], T.e1[:].indirect(T.p16[:, 22:22 + KA]), e1u, e1l)
-    wa = switch(1, T.eg1, 0, NA, ga)
-    wb = switch(1, T.eg1, NA, C, gb)
-    sa = places(1, 0, NA, wa)
-    sb = places(1, NA, C, wb)
-    l1a = copy("v", T.l1[:, 0:KA], T.so[:, C + 15:C + NA:16], sa)
-    l1b = copy("v", T.l1[:, KA:22], T.so[:, C + NA + 15:2 * C:16], sb)
-    gta = fetch(1, HY[1], T.l1[:, 0:KA], 0, NA, l1a, d1u, d1l)
-    gtb = fetch(1, HY[1], T.l1[:, KA:22], NA, NB, l1b)
-    ma = [mix(1, T.l1[:, 0:KA], 0, NA, b, bk, gta, l1a, d1u[b], c1l[b], c1u[b]) for b in range(4)]
-    mb = [mix(1, T.l1[:, KA:22], NA, NB, 0, bk, gtb, l1b)]
-    q_pa = quant("m1", 0, NA, T.mp1[:, 0:4 * NA], ma)
-    copy("a", T.wd[:, 0:C:2], T.wb[:, C:2 * C:2], wa, wb)
-    wd1 = op("a", lambda q: q.activation(T.wd[:, 1:C:2], T.wb[:, C:2 * C:2], ACT.Copy, scale=-1.0))
-    wgu = copy("a", T.wg[:, 160:C], T.wd[:].indirect(T.q16[:, 10:22]), wd1, q16)
-    ba, bz = [4, 5, 6, 7], [0, 1, 2, 3]
-    mms = layer(W, "m1", 0, NA, ba, q_pa)
-    ha = [relu("a", T.mh1, 0, NA, b, ba, mms) for b in range(3)]
-    mb += [mix(1, T.l1[:, KA:22], NA, NB, b, bk, gtb, l1b) for b in range(1, 4)]
-    ha.append(relu("v", T.mh1, 0, NA, 3, ba, mms))
-    q_pb = quant("m1", NA, NB, T.mp1[:, 4 * NA:4 * C], mb)
-    q_ha = quant("h1", 0, NA, T.mh1[:, 0:4 * NA], ha)
-    su = scan(T.sg[:, HALF:C], T.ki[:], T.wg[:, HALF:C], wgu)
-    mwb = layer(W, "m1", NA, NB, ba, q_pb)
-    mza = layer(Z, "h1", 0, NA, bz, q_ha, l_zs, l_zc)
-    wgl = copy("a", T.wg[:, 0:160], T.wd[:].indirect(T.q16[:, 0:10]))
-    hb = [relu("av"[b % 2], T.mh1, NA, NB, b, ba, mwb) for b in range(4)]
-    q_hb = quant("h1", NA, NB, T.mh1[:, 4 * NA:4 * C], hb)
-    tu = tt(T.tg[:, 12:23], T.sg[:, HALF + 15:C:16], T.r1[:, HALF + 15:C:16], ALU.add, su)
-    g1a = [plain("av"[b % 2], T.mg1, 0, NA, b, bz, mza) for b in range(4)]
-    n1u = ts(T.n1[:, 12:23], T.tg[:, 12:23], ci, -512.0, ALU.mult, ALU.add, tu)
-    mzb = layer(Z, "h1", NA, NB, ba, q_hb)
-    g1b = [plain("av"[b % 2], T.mg1, NA, NB, b, ba, mzb) for b in range(4)]
-
-    def undo(engs, X, G, off, a, ga, gb, dep):
-        return [copy(engs[b], X[:, 4 * a + b:4 * (a + HALF):4], G[:, C * b:C * b + C].indirect(off),
-                     ga[b], gb[b], dep) for b in range(4)]
-
-    xu = undo("avav", T.mx1, T.mg1, T.n1[:, 12:23], HALF, g1a, g1b, n1u)
-    q_x = quant("o2", 0, HALF, T.mx1[:, 4 * HALF:4 * C], xu)
-    arr2, left2 = send(2, "o2", "s2", 1, q_x)
-
-    sl = scan(T.sg[:, 0:HALF], T.ki[:], T.wg[:, 0:HALF], wgl)
-    tl = tt(T.tg[:, 0:11], T.sg[:, 15:HALF:16], T.r1[:, 15:HALF:16], ALU.add, sl)
-    n1l = ts(T.n1[:, 0:11], T.tg[:, 0:11], ci, -512.0, ALU.mult, ALU.add, tl)
-    sct0 = copy("v", T.sc0[:].indirect(T.l0[:, 0:11]), T.cnt[:, 0:HALF])
-    xl = undo("aaav", T.mx1, T.mg1, T.n1[:, 0:11], 0, g1a, g1b, n1l)
-    q_x = quant("s2", 0, HALF, T.mx1[:, 0:4 * HALF], xl)
-    bk = [0, 1, 2, 3]
-    mms = layer(Z, "s2", 0, HALF, bk, q_x)
-    sct0 = copy("v", T.sc0[:].indirect(T.l0[:, 12:23]), T.cnt[:, HALF:C], sct0)
-    r0u = scan(T.r0[:, HALF:C], T.ki[:], T.sc0[:, HALF:C], sct0)
-    n0u = ts(T.n0[:, 12:23], T.r0[:, HALF + 15:C:16], ci, -512.0, ALU.mult, ALU.add, r0u)
-    g0l = [plain("a", T.mg0, 0, HALF, b, bk, mms) for b in range(4)]
-    bk = [4, 5, 6, 7]
-    mms = layer(Z, "s2", HALF, HALF, bk, arr2)
-    g0u = [plain("av"[b % 2], T.mg0, HALF, HALF, b, bk, mms) for b in range(4)]
-    xu = undo("avav", T.mx0, T.mg0, T.n0[:, 12:23], HALF, g0l, g0u, n0u)
-    q_x = quant("o3", 0, HALF, T.mx0[:, 4 * HALF:4 * C], xu)
-    arr3, left3 = send(3, "o3", "s3", 0, q_x)
-
-    r0l = scan(T.r0[:, 0:HALF], T.ki[:], T.sc0[:, 0:HALF], sct0)
-    q_v = quant("v", 0, 128, T.vt[:], l_v)
-    n0l = ts(T.n0[:, 0:11], T.r0[:, 15:HALF:16], ci, -512.0, ALU.mult, ALU.add, r0l)
-    f0 = op("a", lambda q: q.activation(T.lf[:, 0:C], T.cnt[:].indirect(T.l0c[:]), ACT.Identity, bias=-512.0), l0c)
-    xl = undo("avav", T.mx0, T.mg0, T.n0[:, 0:11], 0, g0l, g0u, n0l)
-    q_x = quant("s3", 0, HALF, T.mx0[:, 0:4 * HALF], xl)
-    f1 = op("a", lambda q: q.activation(T.lf[:, C:2 * C], T.cnt[:].indirect(T.l1[:]), ACT.Identity, bias=-512.0),
-            l1a, l1b)
+    backward(0, 0, "s2", LO, undo(1, 0, half("s2", 0), inverse1(0)))
+    sct0 = copy("sct00", "v", T.sc0[:].indirect(lst("l0", 0)), T.cnt[:, 0:HALF], l0[0], cnt)
+    sct0 = copy("sct01", "v", T.sc0[:].indirect(lst("l0", 1)), T.cnt[:, HALF:C], l0[1], sct0)
+    r0 = scan("r0", T.r0[:], T.ki[:], T.sc0[:], sct0, ki)
+    n0 = [ts("n0%d" % h, lst("n0", h), T.r0[:, HALF * h + 15:HALF * h + HALF:16], ci, -512.0, ALU.mult, ALU.add, r0)
+          for h in range(2)]
+    backward(0, 1, "s2", HI, arr2)
+    arr3, left3 = send(3, "o3", "s3", 0, undo(0, 1, half("o3", 0), n0[1]))
+    q_x = undo(0, 0, half("s3", 0), n0[0])
+    q_v = quant("qv", pair("v", 0, 128), T.vt[:], l_v)
+    f = [op("f%d%d" % (t, h), "a", lambda q, t=t, h=h: q.activation(
+        T.lf[:, C * t + HALF * h:C * t + HALF * h + HALF], T.cnt[:].indirect(lst("l%d" % t, h)), ACT.Identity,
+        bias=-512.0), (l0, l1)[t][h], cnt) for t in range(2) for h in range(2)]
 
     V = pair("v", 0, 128)
-    yl = evac("v", 0, HALF, T.yb[:, 0:HALF], 1.0, False, mm(0, V, pair("s3", 0, HALF), HALF, q_x, q_v))
-    dma("s", T.oc[:, 0:4 * HALF], T.c_s3[:, 0:HALF].bitcast(dt.uint8), q_x, sem="outs")
-    dma("s", T.y[:, 0:HALF], T.yb[:, 0:HALF], yl, sem="outs")
-    dma("a", T.ol[:], T.lf[0:128:16, :], f0, f1, sem="outa")
-    yu = evac("v", 1, HALF, T.yb[:, HALF:C], 1.0, False, mm(1, V, pair("s3", HALF, C), HALF, arr3))
-    dma("a", T.oc[:, 4 * HALF:4 * C], T.c_s3[:, HALF:C].bitcast(dt.uint8), arr3, sem="outa")
+    mm("sy0", 0, V, half("s3", 0), q_x, q_v)
+    yl = evac("y0", PLAN["y"][0], 0, T.yb[:, 0:HALF])
+    mm("sy1", 1, V, half("s3", 1), arr3, q_v)
+    yu = evac("y1", PLAN["y"][1], 1, T.yb[:, HALF:C])
+    dma("ol", "a", T.ol[:], T.lf[0:128:16, :], f, sem="outa")
+    dma("oc0", "s", T.oc[:, 0:4 * HALF], T.c_s3[:, 0:HALF].bitcast(dt.uint8), q_x, sem="outs")
+    dma("oy0", "s", T.y[:, 0:HALF], T.yb[:, 0:HALF], yl, sem="outs")
+    dma("oc1", "s", T.oc[:, 4 * HALF:4 * C], T.c_s3[:, HALF:C].bitcast(dt.uint8), arr3[0], sem="outs")
     for k in range(4):
-        dma("aaas"[k], T.osc[4 * k:4 * k + 4, :], T.s_s3[32 * k:32 * k + 4, :], arr3, q_x, sem="out" + "aaas"[k])
-    dma("s", T.y[:, HALF:C], T.yb[:, HALF:C], yu, sem="outs")
+        dma("os%d" % k, "a", T.osc[4 * k:4 * k + 4, :], T.s_s3[32 * k:32 * k + 4, :], arr3[1], q_x, sem="outa")
+    dma("oy1", "s", T.y[:, HALF:C], T.yb[:, HALF:C], yu, sem="outs")
 
+    place = {n: i for i, n in enumerate(ORDER.split())}
+    ops.sort(key=lambda o: place[o["name"]])
     for o in ops:
+        o["deps"] = [d for d in o["deps"] if d["kind"] != "r"]
         for d in o["deps"]:
             d["used"] = True
     total = {}
@@ -432,5 +395,5 @@ def rank_program(g, core, T, topo):
             o["clock"] = dict(clock[o["eng"]])
             o["clock"][o["sem"]] = o["val"]
     wait("g", [left2, left3])
-    wait("s", [event("outs", total["outs"])])
-    wait("a", [event("outa", total["outa"])])
+    wait("s", [event("outs", total["outs"], None)])
+    wait("a", [event("outa", total["outa"], None)])

from concourse.mybir import dt, AluOpType, ActivationFunctionType

C, HALF, FAR = 352, 176, (4, 2)
BIG = 2.0 ** 40
F32, BF, I32, U16, Q4, U8 = "float32", "bfloat16", "int32", "uint16", "float8_e4m3fn_x4", "uint8"

PLAN = dict(d00="aaaa", d01="vaaa", d10="aavv", d11="aaaa", e="aavv", ga="avaava", m00="faaa", m01="ffaa", m10="ffaa",
            m11="ffaa", h00="vvaa", h01="aavv", h10="aava", h11="avva", g10="vaaa", g11="vaav", g00="aaaa",
            g01="avav", x10="vaaa", x11="vaav", x00="vvaa", x01="vava", wg="aa", y="vv", c00="gggg", c01="gggg",
            c10="gggg", c11="gggg", first=0, wd="g")
ORDER = """
lxu mz1 ia go lxl lp0 lj00 lj01 lp1 lu ib mz0 iv tx iu k2 cnt0 ip k3 cnt256 k1 cnt128 k4 co k16 e2 kw0 qxu sc0 qe1 ss0
e1 ki qe3 qxl kw1 sd001 d001 p16 mwb qe0 sct1 sd000 sd003 d000 lj10 lj11 c000 qu lws lwc cc qe2 pks pkc sd002 d002 sct2
se00 e00 d003 wslot r1 se01 sd011 sd010 e01 sd012 sd013 pd ga00 ga01 ga02 d010 w01 kslot c010 d011 w00 d012 sn01 d013
sn00 c011 l01 l00 m010 t013 m011 t012 m013 t002 m012 qp01 t001 sc1 m002 ss1 t003 m000 m001 m003 qp00 sw003 sw001 lzc
lzs lv sw002 h003 sw000 h001 h002 h000 qh00 se10 sw011 sw012 e10 sw010 h011 q16 h010 h012 sw013 sd100 h013 sd101 sd102
d100 sd103 qh01 d101 d102 c100 se11 sd111 sd110 e11 sd112 d111 sd113 ga11 c101 ga10 d103 ga12 w10 c111 d113 w11 d110
sn10 d112 sn11 wd0 wd1 l10 l11 t103 m101 c110 t102 m100 m103 t112 m102 wg1 m111 qp10 t113 m110 sw102 wg0 sw100 sw103
m112 sw101 h103 m113 h101 h102 h100 qp11 sg1 sw110 qh10 sw112 sw113 h110 sw111 h112 sz101 sz102 h113 sz100 h111 sz103
g101 tg1 qh11 g102 g100 g103 sz111 sg0 sz113 g111 sz112 sz110 n11 g112 tg0 g113 x111 g110 x113 x112 x110 n10 qx11 x101
x100 sc2 ss2 x102 qv sct00 x103 qx10 sct01 sz001 sz000 sz002 g001 sz003 g000 r0 g003 sz010 sz011 g002 sz012 n01 sz013
n00 g010 g011 g012 g013 x011 x010 x013 x012 x002 qx01 x001 sc3 ss3 x003 x000 f11 qx00 f00 oc0 sy0 f01 y0 oy0 f10 oc1
os2 os0 os3 os1 ol sy1 y1 oy1
"""

SCRATCH = {}
for _n, _w in (("xt", 4 * C), ("ut", 512), ("vt", 512), ("z0", 516), ("z1", 516), ("dh0", 4 * C), ("dh1", 4 * C),
               ("tm0", 4 * C), ("tm1", 4 * C), ("dc0", 4 * C), ("dc1", 4 * C), ("mp0", 4 * C), ("mp1", 4 * C),
               ("mh0", 4 * C), ("mh1", 4 * C), ("mg0", 4 * C), ("mg1", 4 * C), ("mx0", 4 * C), ("mx1", 4 * C)):
    SCRATCH[_n] = ("sbuf", [128, _w], BF)
for _n, _w in (("xi", 64), ("xo", 80), ("iv", 132), ("pcol", 4), ("cc", 4), ("ta", 32), ("tb", 32), ("k16", 32),
               ("kw", 2 * C), ("ki", C), ("wd", C), ("wb", 2 * C), ("so", 2 * C), ("cnt", C), ("df", 44), ("e0", C),
               ("e1", C), ("eg0", C), ("eg1", C), ("sc0", C), ("sc1", C), ("r0", C), ("r1", C), ("wg", C), ("sg", C),
               ("tg", 22), ("lf", 2 * C), ("yb", C)):
    SCRATCH[_n] = ("sbuf", [128, _w], F32)
for _n in ("pi", "pj"):
    SCRATCH[_n] = ("sbuf", [128, 44], I32)
for _n, _w in (("o16", 38), ("p16", 44), ("l0", 24), ("l1", 24), ("n0", 24), ("n1", 24), ("q16", 22)):
    SCRATCH[_n] = ("sbuf", [128, _w], U16)
for _n, _w in (("u", 128), ("up", 256), ("v", 128), ("w", 512), ("z", 512), ("e", 512), ("s0", C), ("o0", HALF),
               ("m0", C), ("o1", HALF), ("s1", C), ("m1", C), ("h1", C), ("s2", C), ("o2", HALF), ("s3", C),
               ("o3", HALF)):
    SCRATCH["c_" + _n] = ("sbuf", [128, _w], Q4)
    SCRATCH["s_" + _n] = ("sbuf", [128, _w], U8)
for _k in range(8):
    SCRATCH["ps%d" % _k] = ("psum", [128, 512], F32)

SEMAPHORES = (["kv", "ka", "kp", "kg", "go", "arrc"] + ["arr%d" % k for k in range(4)]
              + ["left%d" % k for k in range(4)] + ["d%d" % k for k in range(16)] + ["outs", "outa"])


def _flat(x, out):
    for d in x:
        if isinstance(d, (list, tuple)):
            _flat(d, out)
        elif d is not None:
            out.append(d)
    return out


def rank_program(g, core, T, topo):
    rank = T.rank_of(core)
    if rank is None:
        return
    ALU, ACT = AluOpType, ActivationFunctionType
    queue = {"v": g.vector, "a": g.scalar, "p": g.tensor, "g": g, "s": g.sync}
    ops = []

    def op(name, eng, fn, *deps):
        o = {"name": name, "eng": eng, "fn": fn, "deps": _flat(deps, []), "sem": "k" + eng, "kind": "c", "used": False}
        ops.append(o)
        return o

    dmas = [0]

    def dma(name, eng, out, in_, *deps, sem=None):
        if sem is None:
            sem = "d%d" % dmas[0]
            dmas[0] += 1
        o = op(name, eng, lambda q: q.dma_start(out, in_), *deps)
        o.update(sem=sem, kind="d", used=True)
        return o

    def event(sem, val, src):
        return {"sem": sem, "val": val, "clock": {sem: val}, "kind": "e", "used": True, "src": src}

    def pair(name, a, b):
        return T["c_" + name][:, a:b], T["s_" + name][:, a:b]

    def half(name, h):
        return pair(name, HALF * h, HALF * h + HALF)

    def quant(name, dst, tile, *deps):
        return op(name, "v", lambda q: q.quantize_mx(dst[0], dst[1], tile), *deps)

    last = [None] * 8

    def banked(o, bank):
        if last[bank] is not None:
            o["deps"].append(last[bank])
        last[bank] = o
        return o

    def mm(name, bank, lhs, rhs, *deps):
        out = T["ps%d" % bank][:, 0:HALF]
        return banked(op(name, "p", lambda q: q.matmul_mx(out, lhs[0], lhs[1], rhs[0], rhs[1], True, True), *deps), bank)

    def evac(name, eng, bank, out, scale=1.0, relu=False):
        src = T["ps%d" % bank][:, 0:HALF]
        if eng == "a":
            f = ACT.Relu if relu else ACT.Copy
            o = op(name, "a", lambda q: q.activation(out, src, f, scale=scale))
        elif relu:
            o = op(name, "v", lambda q: q.tensor_scalar(out, src, 0.0, scale, ALU.max, ALU.mult))
        elif scale == 1.0:
            o = op(name, "v", lambda q: q.tensor_copy(out, src))
        else:
            o = op(name, "v", lambda q: q.tensor_scalar(out, src, scale, None, ALU.mult))
        return banked(o, bank)

    def copy(name, eng, out, in_, *deps):
        if eng == "g":
            return op(name, "g", lambda q: q.affine_select(out, in_, [[0, HALF]], ALU.is_ge, 0.0, 0, 0), *deps)
        if eng == "a":
            return op(name, "a", lambda q: q.activation(out, in_, ACT.Copy), *deps)
        return op(name, "v", lambda q: q.tensor_copy(out, in_), *deps)

    def times(name, out, in_, scale, *deps):
        return op(name, "a", lambda q: q.activation(out, in_, ACT.Copy, scale=scale), *deps)

    def ts(name, out, in0, s1, s2, o0, o1, *deps):
        if o1 is None:
            return op(name, "v", lambda q: q.tensor_scalar(out, in0, s1, None, o0), *deps)
        return op(name, "v", lambda q: q.tensor_scalar(out, in0, s1, s2, o0, o1), *deps)

    def tt(name, out, in0, in1, o, *deps):
        return op(name, "v", lambda q: q.tensor_tensor(out, in0, in1, o), *deps)

    def scan(name, out, k, x, *deps):
        return op(name, "v", lambda q: q.tensor_tensor_scan(out, k, x, 0.0, ALU.mult, ALU.add), *deps)

    def fill(name, ap):
        return op(name, "v", lambda q: q.memset(ap, 0.0))

    def iota(name, out, pattern, base, cm, *deps):
        return op(name, "g", lambda q: q.iota(out, pattern, base, cm, allow_small_or_imprecise_dtypes=True), *deps)

    def send(k, src, dst, t, dep):
        d = FAR[t]
        peer = T.cores[rank + d if (rank // d) % 2 == 0 else rank - d]
        rid, pid = topo.addr(peer, core)
        mask = topo.mask(core, peer)
        n = len(topo.engines(core, peer))
        (sc, ss), (dc, ds) = half(src, 0), half(dst, 1)
        arr, left = T.sem["arr%d" % k], T.sem["left%d" % k]
        arrc = T.sem.arrc if k == 3 else arr
        a = op("sc%d" % k, "g", lambda q: q.remote_dma(dc.bitcast(dt.uint8), sc.bitcast(dt.uint8), arrc, left, pid, rid,
                                                       mask), dep)
        b = op("ss%d" % k, "g", lambda q: q.remote_dma(ds, ss, arr, left, pid, rid, mask))
        a["kind"] = b["kind"] = "r"
        b["deps"].append(a)
        if k == 3:
            return [event("arrc", n, a), event("arr3", n, b)], event("left3", 2 * n, b)
        return event("arr%d" % k, 2 * n, b), event("left%d" % k, 2 * n, b)

    W = [pair("w", 128 * b, 128 * b + 128) for b in range(4)]
    Z = [pair("z", 128 * b, 128 * b + 128) for b in range(4)]
    E = [pair("e", 128 * b, 128 * b + 128) for b in range(4)]
    U = [pair("up", 128 * t, 128 * t + 128) for t in range(2)]

    l_xu = dma("lxu", "s", T.xt[:, 4 * HALF:4 * C], T.x[:, 4 * HALF:4 * C])
    go = op("go", "s", lambda q: q.sem_inc(T.sem.go, 1), {"kind": "r", "src": l_xu})
    go["kind"] = "r"
    l_p0 = dma("lp0", "s", T.pi[:, 0:22], T.p0[:], go)
    l_xl = dma("lxl", "s", T.xt[:, 0:4 * HALF], T.x[:, 0:4 * HALF], go)
    l_p1 = dma("lp1", "a", T.pi[:, 22:44], T.p1[:], event("go", 1, go))
    l_u = dma("lu", "a", T.ut[:], T.u[:], event("go", 1, go))

    i_a = iota("ia", T.xi[:, 0:32], [[0, 2], [2, 8], [0, 2]], 1, 0)
    i_b = iota("ib", T.xi[:, 32:64], [[0, 2], [1, 16]], 0, 0)
    i_v = iota("iv", T.iv[:, 0:130], [[1, 130]], -1, 0)
    i_p = iota("ip", T.pcol[:, 0:1], [[0, 1]], 0, 1)
    i_u = iota("iu", T.xo[:, 64:80], [[1, 2], [16, 8]], 0, 0)

    q_xu = quant("qxu", half("o0", 0), T.xt[:, 4 * HALF:4 * C], l_xu)
    arr0, left0 = send(0, "o0", "s0", 0, q_xu)

    m_z0, m_z1 = fill("mz0", T.z0[:]), fill("mz1", T.z1[:])
    m_wb = iota("mwb", T.wb[:, 1:2 * C:2], [[0, C]], 0, 0, left0["src"])
    t_x = op("tx", "v", lambda q: q.transpose(T.xo[:, 0:64], T.xi[:]), i_a, i_b)
    s1, pm = T.xo[:, 31:32], T.xo[:, 32:33]
    c_o = copy("co", "v", T.o16[:], T.xo[:, 42:80], t_x, i_u)
    k1 = ts("k1", T.ta[:, 0:16], T.iv[:, 1:17], s1, BIG, ALU.is_equal, ALU.mult, t_x, i_v)
    k2 = ts("k2", T.tb[:, 0:16], T.iv[:, 2:18], s1, None, ALU.not_equal, None, t_x, i_v)
    k3 = ts("k3", T.ta[:, 16:32], T.iv[:, 0:16], pm, BIG, ALU.is_equal, ALU.mult, t_x, i_v)
    k4 = ts("k4", T.tb[:, 16:32], T.iv[:, 1:17], pm, None, ALU.not_equal, None, t_x, i_v)
    c_c = ts("cc", T.cc[:, 0:2], T.xo[:, 31:33], 15.0, 1.0 / BIG, ALU.is_equal, ALU.max, t_x)
    k16 = tt("k16", T.k16[:], T.ta[:], T.tb[:], ALU.max, k1, k2, k3, k4)
    cw, ci = T.cc[:, 0:1], T.cc[:, 1:2]
    e1 = ts("e1", T.z0[:, 2:514:4], T.iv[:, 1:129], T.pcol[:, 0:1], 0.5, ALU.is_equal, ALU.mult, i_v, i_p, m_z0)
    e2 = ts("e2", T.z1[:, 3:515:4], T.iv[:, 1:129], T.pcol[:, 0:1], 0.5, ALU.is_equal, ALU.mult, i_v, i_p, m_z1)
    q_e = [quant("qe%d" % b, E[b], (T.z0, T.z1)[b % 2][:, 2 - 2 * (b // 2):514 - 2 * (b // 2)], (e1, e2)[b % 2])
           for b in range(4)]
    cnt = []
    for a, n in ((0, 128), (128, 128), (256, 96)):
        cnt.append(op("cnt%d" % a, "a", lambda q, a=a, n=n: q.activation(
            T.cnt[:, a:a + n], T.iv[:, 1:1 + n], ACT.Identity, bias=float(512 + a)), i_v))
    kw0 = copy("kw0", "a", T.kw[:, 0:C], T.k16[:, 0:16].indirect(T.o16[:, 0:22]), k16, c_o)
    ki = copy("ki", "a", T.ki[:], T.k16[:, 16:32].indirect(T.o16[:, 0:22]), k16, c_o)
    kw1 = copy("kw1", "a", T.kw[:, C:2 * C], T.kw[:, 0:C], kw0)
    l_pj = [dma("lj%d%d" % (t, k), "sa"[t], T.pj[k:128:2, 22 * t:22 * t + 22], (T.p0, T.p1)[t][1 - k:128:2, :],
                (go, event("go", 1, go))[t]) for t in range(2) for k in range(2)]
    p16 = copy("p16", "v", T.p16[:], T.pi[:], l_p0, l_p1)
    p_d = tt("pd", T.df[:], T.pj[:], T.pi[:], ALU.subtract, l_pj, l_p0, l_p1)
    kslot = times("kslot", T.kw[:, 15:2 * C:16], T.df[:], cw, p_d, kw1, c_c)
    wslot = copy("wslot", "v", T.wb[:, 15:2 * C:16], T.pi[:], l_p0, l_p1, m_wb)

    q_xl = quant("qxl", half("s0", 0), T.xt[:, 0:4 * HALF], l_xl)
    q_u = quant("qu", pair("u", 0, 128), T.ut[:], l_u)
    uo = T.o16[:, 22:38]
    pk = [op("pkc", "v", lambda q: q.tensor_copy(T.c_up[:].bitcast(dt.uint32),
                                                 T.c_u[:].bitcast(dt.uint32).indirect(uo)), q_u, c_o),
          copy("pks", "a", T.s_up[:], T.s_u[:].indirect(uo), q_u, c_o)]
    sct1 = copy("sct1", "v", T.sc1[:].indirect(T.p16[:, 22:34]), T.cnt[:, 0:192], p16, cnt)
    sct1 = copy("sct2", "v", T.sc1[:].indirect(T.p16[:, 34:44]), T.cnt[:, 192:C], sct1)
    r1 = scan("r1", T.r1[:], T.ki[:], T.sc1[:], sct1, ki)
    q16 = ts("q16", T.q16[:], T.r1[:, 15:C:16], ci, -512.0, ALU.mult, ALU.add, r1, c_c)

    l_ws = dma("lws", "s", T.s_w[:], T.ws[:], left0)
    l_wc = dma("lwc", "s", T.c_w[:].bitcast(dt.uint8), T.wc[:], left0)

    ev, dv, at = {}, {}, {}

    def unpack(t, h, S, sb, banks, dep):
        a = HALF * h
        mm("se%d%d" % (t, h), sb, U[t], half(S, h), dep, pk)
        ev[t, h] = evac("e%d%d" % (t, h), PLAN["e"][2 * t + h], sb, T["e%d" % t][:, a:a + HALF])
        for b in range(4):
            mm("sd%d%d%d" % (t, h, b), banks[b], E[b], half(S, h), dep, q_e[b])
            dv[t, h, b] = evac("d%d%d%d" % (t, h, b), PLAN["d%d%d" % (t, h)][b], banks[b],
                               T["dh%d" % t][:, C * b + a:C * b + a + HALF])
            at[t, h, b] = banks[b]

    def lst(name, h):
        return T[name][:, 12 * h:12 * h + 11]

    def lists(t, first):
        e, eg, out, done = T["e%d" % t], T["eg%d" % t], [None, None], []
        cut = ((0, 6), (6, 12), (12, 22)) if first == 0 else ((10, 16), (16, 22), (0, 10))
        ga = [copy("ga%d%d" % (t, k), PLAN["ga"][3 * t + k], eg[:, 16 * c0:16 * c1],
                   e[:].indirect(T.p16[:, 22 * t + c0:22 * t + c1]), ev[t, 0], ev[t, 1], p16)
              for k, (c0, c1) in enumerate(cut)]
        for h, (c0, c1), got in ((first, (cut[0][0], cut[1][1]), ga[:2]), (1 - first, cut[2], ga[2])):
            done.append(tt("w%d%d" % (t, h), T.wb[:, C * t + 16 * c0:C * t + 16 * c1:2], eg[:, 16 * c0 + 1:16 * c1:2],
                           eg[:, 16 * c0:16 * c1:2], ALU.is_gt, got))
            a = C * t + HALF * h
            sc = scan("sn%d%d" % (t, h), T.so[:, a:a + HALF], T.kw[:, a:a + HALF], T.wb[:, a:a + HALF], done,
                      kslot, wslot)
            out[h] = copy("l%d%d" % (t, h), "v", lst("l%d" % t, h), T.so[:, a + 15:a + HALF:16], sc)
        return out, done

    def mix(t, h, dst, l):
        a, off, dh, done = HALF * h, lst("l%d" % t, h), T["dh%d" % t], []
        for b in range(4):
            out, win, name = T["mp%d" % t][:, 4 * a + b:4 * (a + HALF):4], dh[:, C * b:C * b + C], "%d%d%d" % (t, h, b)
            if PLAN["m%d%d" % (t, h)][b] == "f":
                dc = T["dc%d" % t][:, C * b + a:C * b + a + HALF]
                c = copy("c" + name, PLAN["c%d%d" % (t, h)][b], dc, dh[:, C * b + a:C * b + a + HALF], dv[t, h, b])
                done.append(tt("m" + name, out, win.indirect(off), dc, ALU.add, l, c, dv[t, 0, b], dv[t, 1, b]))
            else:
                tm = T["tm%d" % t][:, C * b + a:C * b + a + HALF]
                got = copy("t" + name, "a", tm, win.indirect(off), l, dv[t, 0, b], dv[t, 1, b])
                done.append(banked(tt("m" + name, out, tm, T["ps%d" % at[t, h, b]][:, 0:HALF], ALU.add, got),
                                   at[t, h, b]))
        return quant("qp%d%d" % (t, h), dst, T["mp%d" % t][:, 4 * a:4 * (a + HALF)], done)

    def forward(t, h, src, dst, banks, *deps):
        a, H, done = HALF * h, T["mh%d" % t], []
        for b in range(4):
            mm("sw%d%d%d" % (t, h, b), banks[b], W[b], half(src, h), *deps)
            done.append(evac("h%d%d%d" % (t, h, b), PLAN["h%d%d" % (t, h)][b], banks[b],
                             H[:, 4 * a + b:4 * (a + HALF):4], 0.03125, True))
        return quant("qh%d%d" % (t, h), half(dst, h), H[:, 4 * a:4 * (a + HALF)], done)

    gv = {}

    def backward(t, h, src, banks, *deps):
        a = HALF * h
        for b in range(4):
            mm("sz%d%d%d" % (t, h, b), banks[b], Z[b], half(src, h), *deps)
            gv[t, h, b] = evac("g%d%d%d" % (t, h, b), PLAN["g%d%d" % (t, h)][b], banks[b],
                               T["mg%d" % t][:, C * b + a:C * b + a + HALF], 0.03125)

    def undo(t, h, dst, n):
        a, X, G = HALF * h, T["mx%d" % t], T["mg%d" % t]
        done = [copy("x%d%d%d" % (t, h, b), PLAN["x%d%d" % (t, h)][b], X[:, 4 * a + b:4 * (a + HALF):4],
                     G[:, C * b:C * b + C].indirect(lst("n%d" % t, h)), n, gv[t, 0, b], gv[t, 1, b]) for b in range(4)]
        return quant("qx%d%d" % (t, h), dst, X[:, 4 * a:4 * (a + HALF)], done)

    LO, HI = (0, 1, 2, 3), (5, 6, 7, 4)
    unpack(0, 0, "s0", 4, LO, q_xl)
    unpack(0, 1, "s0", 4, (5, 6, 7, 0), arr0)
    l0, w0 = lists(0, 1)
    arr1, left1 = send(1, "o1", "m0", 1, mix(0, 1, half("o1", 0), l0[1]))
    q_pl = mix(0, 0, half("m0", 0), l0[0])
    l_zs = dma("lzs", "s", T.s_z[:], T.zs[:], left1)
    l_zc = dma("lzc", "s", T.c_z[:].bitcast(dt.uint8), T.zc[:], left1)
    l_v = dma("lv", "s", T.vt[:], T.v[:], left1)
    unpack(1, 0, "s1", 4, LO, forward(0, 0, "m0", "s1", (4, 5, 6, 7), q_pl, l_ws, l_wc))
    unpack(1, 1, "s1", 0, HI, forward(0, 1, "m0", "s1", HI, arr1, l_ws, l_wc))

    fst = PLAN["first"]
    l1, w1 = lists(1, fst)
    q_p = {h: mix(1, h, half("m1", h), l1[h]) for h in (fst, 1 - fst)}
    q_h = {h: forward(1, h, "m1", "h1", (LO, HI)[h], q_p[h]) for h in (fst, 1 - fst)}
    for h in (fst, 1 - fst):
        backward(1, h, "h1", (LO, HI)[h], q_h[h], l_zs, l_zc)
    wd = [copy("wd0", PLAN["wd"], T.wd[:, 0:C:2], T.wb[:, C:2 * C:2], w1),
          times("wd1", T.wd[:, 1:C:2], T.wb[:, C:2 * C:2], -1.0, w1)]
    wg = [copy("wg0", PLAN["wg"][0], T.wg[:, 0:160], T.wd[:].indirect(T.q16[:, 0:10]), wd, q16),
          copy("wg1", PLAN["wg"][1], T.wg[:, 160:C], T.wd[:].indirect(T.q16[:, 10:22]), wd, q16)]

    def inverse1(h):
        a, c = HALF * h, slice(11 * h, 11 * h + 11)
        s = scan("sg%d" % h, T.sg[:, a:a + HALF], T.ki[:, 0:HALF], T.wg[:, a:a + HALF], wg[h:])
        s = tt("tg%d" % h, T.tg[:, c], T.sg[:, a + 15:a + HALF:16], T.r1[:, a + 15:a + HALF:16], ALU.add, s)
        return ts("n1%d" % h, lst("n1", h), T.tg[:, c], ci, -512.0, ALU.mult, ALU.add, s)

    arr2, left2 = send(2, "o2", "s2", 1, undo(1, 1, half("o2", 0), inverse1(1)))

    backward(0, 0, "s2", LO, undo(1, 0, half("s2", 0), inverse1(0)))
    sct0 = copy("sct00", "v", T.sc0[:].indirect(lst("l0", 0)), T.cnt[:, 0:HALF], l0[0], cnt)
    sct0 = copy("sct01", "v", T.sc0[:].indirect(lst("l0", 1)), T.cnt[:, HALF:C], l0[1], sct0)
    r0 = scan("r0", T.r0[:], T.ki[:], T.sc0[:], sct0, ki)
    n0 = [ts("n0%d" % h, lst("n0", h), T.r0[:, HALF * h + 15:HALF * h + HALF:16], ci, -512.0, ALU.mult, ALU.add, r0)
          for h in range(2)]
    backward(0, 1, "s2", HI, arr2)
    arr3, left3 = send(3, "o3", "s3", 0, undo(0, 1, half("o3", 0), n0[1]))
    q_x = undo(0, 0, half("s3", 0), n0[0])
    q_v = quant("qv", pair("v", 0, 128), T.vt[:], l_v)
    f = [op("f%d%d" % (t, h), "a", lambda q, t=t, h=h: q.activation(
        T.lf[:, C * t + HALF * h:C * t + HALF * h + HALF], T.cnt[:].indirect(lst("l%d" % t, h)), ACT.Identity,
        bias=-512.0), (l0, l1)[t][h], cnt) for t in range(2) for h in range(2)]

    V = pair("v", 0, 128)
    mm("sy0", 0, V, half("s3", 0), q_x, q_v)
    yl = evac("y0", PLAN["y"][0], 0, T.yb[:, 0:HALF])
    mm("sy1", 1, V, half("s3", 1), arr3, q_v)
    yu = evac("y1", PLAN["y"][1], 1, T.yb[:, HALF:C])
    dma("ol", "a", T.ol[:], T.lf[0:128:16, :], f, sem="outa")
    dma("oc0", "s", T.oc[:, 0:4 * HALF], T.c_s3[:, 0:HALF].bitcast(dt.uint8), q_x, sem="outs")
    dma("oy0", "s", T.y[:, 0:HALF], T.yb[:, 0:HALF], yl, sem="outs")
    dma("oc1", "s", T.oc[:, 4 * HALF:4 * C], T.c_s3[:, HALF:C].bitcast(dt.uint8), arr3[0], sem="outs")
    for k in range(4):
        dma("os%d" % k, "a", T.osc[4 * k:4 * k + 4, :], T.s_s3[32 * k:32 * k + 4, :], arr3[1], q_x, sem="outa")
    dma("oy1", "s", T.y[:, HALF:C], T.yb[:, HALF:C], yu, sem="outs")

    place = {n: i for i, n in enumerate(ORDER.split())}
    ops.sort(key=lambda o: place[o["name"]])
    for o in ops:
        o["deps"] = [d for d in o["deps"] if d["kind"] != "r"]
        for d in o["deps"]:
            d["used"] = True
    total = {}
    for o in ops:
        if o["kind"] == "d":
            total[o["sem"]] = total.get(o["sem"], 0) + 16
            o["val"] = total[o["sem"]]
        elif o["kind"] == "c" and o["used"]:
            total[o["sem"]] = total.get(o["sem"], 0) + 1
            o["val"] = total[o["sem"]]
    clock = {k: {} for k in queue}

    def wait(eng, deps):
        need = {}
        for d in deps:
            if d["sem"] not in need or need[d["sem"]]["val"] < d["val"]:
                need[d["sem"]] = d
        need = list(need.values())
        for d in need:
            if clock[eng].get(d["sem"], 0) >= d["val"]:
                continue
            if any(x is not d and x["clock"].get(d["sem"], 0) >= d["val"] for x in need):
                continue
            queue[eng].wait_ge(T.sem[d["sem"]], d["val"])
        for d in need:
            for s, v in d["clock"].items():
                clock[eng][s] = max(clock[eng].get(s, 0), v)

    for o in ops:
        wait(o["eng"], o["deps"])
        ins = o["fn"](queue[o["eng"]])
        if o["kind"] != "r" and o["used"]:
            ins.then_inc(T.sem[o["sem"]], 16 if o["kind"] == "d" else 1)
            o["clock"] = dict(clock[o["eng"]])
            o["clock"][o["sem"]] = o["val"]
    wait("g", [left2, left3])
    wait("s", [event("outs", total["outs"], None)])
    wait("a", [event("outa", total["outa"], None)])
